import numpy as np
import ml_dtypes


def mxq(x, axis, fmt="e4m3"):
    dtype, down = {"e4m3": (ml_dtypes.float8_e4m3fn, 7), "e5m2": (ml_dtypes.float8_e5m2, 14)}[fmt]
    v = np.moveaxis(np.asarray(x, np.float32).astype(ml_dtypes.bfloat16).astype(np.float64), axis, -1)
    blocks = v.reshape(v.shape[:-1] + (-1, 32))
    amax = np.abs(blocks).max(-1, keepdims=True)
    byte = np.maximum(np.where(amax > 0, np.frexp(amax)[1] - 1 + 127, 0) - down, 1)
    scale = np.exp2(byte - 127.0)
    codes = (blocks / scale).astype(np.float32).astype(dtype).astype(np.float64)
    return np.moveaxis((codes * scale).reshape(v.shape), -1, axis)


WIDE = False


def mx_kscale(k):
    if not WIDE:
        return np.ones(k)
    levels = np.array([10, -10, 5, -5, 0])
    if k % 512:
        return np.exp2(np.random.permutation(np.resize(levels, k // 32))).repeat(32)
    a = np.empty((k // 512, 16))
    for p in range(k // 512):
        a[p, :8] = np.random.permutation(np.resize(levels, 8))
        for g in range(8):
            far = levels[np.abs(levels - a[p, g]) >= 10]
            a[p, g + 8] = far[np.random.randint(len(far))]
    return np.exp2(a.ravel()).repeat(32)


def f64(x):
    return np.asarray(x).astype(np.float64)


def striped(idx):
    return np.tile(idx.reshape(-1, 16).T, (8, 1)).astype(np.uint16)


def unstriped(offs):
    return offs[:16].T.reshape(-1).astype(np.int64)


E2M1 = np.array([0.0, 0.5, 1.0, 1.5, 2.0, 3.0, 4.0, 6.0, -0.0, -0.5, -1.0, -1.5, -2.0, -3.0, -4.0, -6.0])


def pack_weight(w, fmt):
    k, n = w.shape
    w = f64(np.asarray(w, np.float32).astype(ml_dtypes.bfloat16)).reshape(k // 32, 32, n)
    amax = np.abs(w).max(1)
    if fmt == "e4m3":
        byte = np.frexp(amax)[1] - 1 + 127 - 7
    else:
        mant, ex = np.frexp(amax / 6.0)
        byte = np.where(mant > 0.5, ex, ex - 1) + 127
    byte = np.clip(np.where(amax > 0, byte, 1), 1, 254)
    scaled = (w * np.exp2(127.0 - byte)[:, None, :]).reshape(k, n).astype(np.float32)
    by_word = np.ascontiguousarray(scaled.reshape(k // 512, 128, 4, n).transpose(0, 1, 3, 2))
    if fmt == "e4m3":
        words = by_word.astype(ml_dtypes.float8_e4m3fn).view(np.uint8)
    else:
        c = by_word.astype(ml_dtypes.float4_e2m1fn).view(np.uint8) & 0xF
        words = (c[..., 0::2] | (c[..., 1::2] << 4)).reshape(k // 512, 128, 2 * n)
    return np.ascontiguousarray(words), np.ascontiguousarray(byte.astype(np.uint8).reshape(k // 512, 16, n))


def unpack_weight(words, scales, fmt):
    g, _, n = scales.shape
    words = np.ascontiguousarray(words).reshape(g, 128, n, -1)
    if fmt == "e4m3":
        vals = words.view(ml_dtypes.float8_e4m3fn).astype(np.float64)
    else:
        nib = np.empty((g, 128, n, 4), np.uint8)
        nib[..., 0::2] = words & 0xF
        nib[..., 1::2] = words >> 4
        vals = E2M1[nib]
    vals = vals * np.repeat(np.exp2(scales.astype(np.float64) - 127.0), 8, axis=1)[..., None]
    return vals.transpose(0, 1, 3, 2).reshape(g * 512, n)


def gelu(v):
    return 0.5 * v * (1.0 + np.tanh(np.sqrt(2.0 / np.pi) * (v + 0.044715 * v**3)))


K, K2, C, H, N, T, T2, S = 1024, 512, 512, 1024, 768, 4096, 2048, 1024

def setup_inputs():
    n = np.random.standard_normal
    s, s2 = mx_kscale(K)[:, None], mx_kscale(K2)[:, None]
    sc, u = mx_kscale(C)[:, None], mx_kscale(H)[:, None]
    tab_words, tab_scales = pack_weight(n((K, T)) * s, "e4m3")
    tab2_words, tab2_scales = pack_weight(n((K2, T2)) * s2, "e4m3")
    w2_words, w2_scales = pack_weight(n((K2, H)) / np.sqrt(K2) / s2 * u.T, "e2m1")
    wi_words, wi_scales = pack_weight(n((H, N)) / np.sqrt(H) / u, "e4m3")
    return {
        "tab_words": tab_words, "tab_scales": tab_scales,
        "offs": striped(np.random.permutation(T)[:S]),
        "tab2_words": tab2_words, "tab2_scales": tab2_scales,
        "offs2": striped(np.random.permutation(T2)[:S]),
        "ctx": (n((C, S)) * sc).astype(np.float32),
        "w1": (n((K, H)) / np.sqrt(K) / s * u.T).astype(np.float32),
        "w2_words": w2_words, "w2_scales": w2_scales,
        "wg": (n((C, H)) / np.sqrt(C) / sc).astype(np.float32),
        "wi_words": wi_words, "wi_scales": wi_scales,
        "bi": (0.5 * n(N)).astype(np.float32),
    }

def reference(tab_words, tab_scales, offs, tab2_words, tab2_scales, offs2, ctx, w1,
              w2_words, w2_scales, wg, wi_words, wi_scales, bi):
    v = unpack_weight(tab_words, tab_scales, "e4m3")[:, unstriped(offs)]
    v2 = unpack_weight(tab2_words, tab2_scales, "e4m3")[:, unstriped(offs2)]
    w2 = unpack_weight(w2_words, w2_scales, "e2m1")
    wi = unpack_weight(wi_words, wi_scales, "e4m3")
    a = mxq(f64(w1), 0, "e4m3").T @ v
    d = w2.T @ v2
    c = mxq(f64(wg), 0, "e4m3").T @ mxq(f64(ctx), 0, "e4m3")
    h = (a - d) * (1.0 / (1.0 + np.exp(-c)))
    y = wi.T @ mxq(h, 0, "e4m3")
    return y + f64(bi)[:, None]

@@ -1,0 +1,399 @@
+from contextlib import ExitStack
+
+import concourse.mybir as mybir
+
+K, K2, C, H, N, T, T2, S = 1024, 512, 512, 1024, 768, 4096, 2048, 1024
+FLOPS = 2 * S * (K * H + K2 * H + C * H + H * N)
+F32, BF16 = mybir.dt.float32, mybir.dt.bfloat16
+I32, U32, U16, U8 = mybir.dt.int32, mybir.dt.uint32, mybir.dt.uint16, mybir.dt.uint8
+FP8X4, FP4X4 = mybir.dt.float8_e4m3fn_x4, mybir.dt.float4_e2m1fn_x4
+ACT, ALU = mybir.ActivationFunctionType, mybir.AluOpType
+P = 128
+SCALEQ = "gpsimd"
+PLAN = [
+    ('load', 'list2'),
+    ('load', 'list1'),
+    ('load', 'tab2s'),
+    ('load', 'w2s'),
+    ('load', 'bias'),
+    ('load', 'tabs'),
+    ('load', 'wis'),
+    ('load', 'w110'),
+    ('load', 'w2'),
+    ('load', 'tab2'),
+    ('load', 'tab0'),
+    ('load', 'w10'),
+    ('load', 'tab1'),
+    ('load', 'wg0'),
+    ('load', 'ctx0'),
+    ('load', 'w111'),
+    ('load', 'wg1'),
+    ('load', 'ctx1'),
+    ('load', 'wi'),
+    ('gather', 'tabs', 1),
+    ('gather', 'tab2s', 0),
+    ('cast', 'w110', [('s', 80), ('v', 128)]),
+    ('quant', 'w110'),
+    ('gather', 'tab2s', 1),
+    ('gather', 'tab0', 1),
+    ('gather', 'tab2', 0),
+    ('cast', 'w100', [('s', 64), ('v', 128)]),
+    ('cast', 'w101', [('s', 96), ('v', 128)]),
+    ('quant', 'w100'),
+    ('pre', 0, 1, 'a0', True, False),
+    ('perm',),
+    ('gather', 'tab2', 1),
+    ('gather', 'tab0', 0),
+    ('quant', 'w101'),
+    ('gather', 'tabs', 0),
+    ('pre', 0, 1, 'd', False, False),
+    ('cast', 'ctx0', [('s', 64), ('v', 128)]),
+    ('cast', 'w111', [('s', 48), ('v', 128)]),
+    ('cast', 'wg0', [('s', 80), ('v', 128)]),
+    ('quant', 'wg0'),
+    ('gather', 'tab1', 1),
+    ('pre', 0, 1, 'a1', False, True),
+    ('store', 0, 1, 'svsv'),
+    ('quant', 'ctx0'),
+    ('c', 0, 0),
+    ('c', 0, 3),
+    ('c', 0, 2),
+    ('gather', 'tab1', 0),
+    ('pre', 0, 0, 'a1', True, False),
+    ('pre', 0, 0, 'a0', False, False),
+    ('cast', 'ctx1', [('s', 48), ('v', 128)]),
+    ('quant', 'w111'),
+    ('adm', 1, 2),
+    ('adm', 1, 3),
+    ('adm', 1, 4),
+    ('pre', 0, 0, 'd', False, True),
+    ('store', 0, 0, 'svsv'),
+    ('hst', 0, 0, 'v'),
+    ('hst', 0, 3, 'v'),
+    ('hst', 0, 2, 'v'),
+    ('adm', 1, 1),
+    ('cast', 'wg1', [('s', 80), ('v', 128)]),
+    ('quant', 'wg1'),
+    ('c', 1, 0),
+    ('c', 0, 1),
+    ('hst', 0, 1, 'v'),
+    ('c', 1, 1),
+    ('adm', 1, 5),
+    ('c', 1, 2),
+    ('c', 1, 3),
+    ('adm', 1, 0),
+    ('quant', 'ctx1'),
+    ('c', 0, 6),
+    ('c', 0, 5),
+    ('hq', 0, 3),
+    ('hq', 0, 0),
+    ('ad', 1, 1),
+    ('ad', 1, 0),
+    ('hq', 0, 2),
+    ('ad', 1, 3),
+    ('c', 0, 7),
+    ('hq', 0, 1),
+    ('ad', 1, 2),
+    ('adm', 1, 6),
+    ('c', 0, 4),
+    ('hq', 1, 1),
+    ('hst', 0, 4, 'v'),
+    ('c', 1, 7),
+    ('hq', 1, 3),
+    ('c', 1, 6),
+    ('hq', 1, 0),
+    ('ad', 1, 6),
+    ('hst', 0, 5, 'v'),
+    ('c', 1, 5),
+    ('adm', 1, 7),
+    ('c', 1, 4),
+    ('hq', 1, 2),
+    ('ad', 1, 4),
+    ('y', 0, 512, 'ssvvss', 1),
+    ('hq', 0, 4),
+    ('ad', 1, 5),
+    ('hq', 1, 5),
+    ('hq', 0, 5),
+    ('hq', 1, 4),
+    ('y', 512, 256, 'ssssvv', 2),
+    ('hq', 1, 6),
+    ('ad', 1, 7),
+    ('hst', 0, 7, 'v'),
+    ('hst', 0, 6, 'v'),
+    ('hq', 0, 6),
+    ('hq', 1, 7),
+    ('hq', 0, 7),
+    ('y', 768, 256, 'sssvvv', 2),
+]
+SIGBUFS = 8
+PSB = {"c": 2, "ad": 3, "y": 3}
+ONEPOOL = False
+YBUFS = 6
+CTXW = 512
+GBUFS = 3
+HBUFS = 4
+ABUFS = 2
+FULL = ('w10',)
+
+
+def tile_list_session_shift_recommender_kernel(tc, tab_words, tab_scales, offs, tab2_words, tab2_scales, offs2, ctx, w1,
+                                                        w2_words, w2_scales, wg, wi_words, wi_scales, bi, out):
+    nc = tc.nc
+    with ExitStack() as es:
+        keep = es.enter_context(tc.tile_pool(name="keep", bufs=1))
+        psum = es.enter_context(tc.psum_pool(name="psum", bufs=1))
+        eng = {"v": nc.vector, "s": nc.scalar, "g": nc.gpsimd}
+        sq = {"gpsimd": nc.gpsimd, "sync": nc.sync, "scalar": nc.scalar}[SCALEQ]
+
+        def kt(shape, dt, name):
+            return keep.tile(shape, dt, name=name, align_bytes=64)
+
+        free_banks = [psum.tile([P, 512], F32, name="bank%d" % i) for i in range(8)]
+        rings = {}
+
+        def bank(kind):
+            return free_banks.pop(0)
+
+        def ring(name, n, shape, dt):
+            if name not in rings:
+                rings[name] = [kt(shape, dt, "%s_%d" % (name, i)) for i in range(n)]
+            rings[name].append(rings[name].pop(0))
+            return rings[name][-1]
+
+        list1 = keep.tile([P, S // 16], U16, name="list1")
+        list2 = keep.tile([P, S // 16], U16, name="list2")
+        tabw = [kt([P, T], I32, "tabw%d" % a) for a in range(2)]
+        tabs = kt([P, T // 4], I32, "tabs")
+        tab2w = kt([P, T2], I32, "tab2w")
+        tab2s = kt([P, T2 // 4], I32, "tab2s")
+        w2raw = kt([P, H // 2], I32, "w2raw")
+        w2sraw = kt([P, H // 4], I32, "w2sraw")
+        w2c = kt([P, 2 * H], U8, "w2c")
+        w2s = kt([P, H], U8, "w2s")
+        wiw = kt([P, 2, N], I32, "wiw")
+        wis = kt([P, 2, N // 4], I32, "wis")
+        bias = kt([P, N // P], F32, "bias")
+        vw = [[kt([P, 512], U32, "vw%d%d" % (a, jh)) for jh in range(2)] for a in range(2)]
+        vs = [kt([P, 512], U8, "vs%d" % jh) for jh in range(2)]
+        v2w = [kt([P, 512], U32, "v2w%d" % jh) for jh in range(2)]
+        v2s = [kt([P, 512], U8, "v2s%d" % jh) for jh in range(2)]
+        hc = [kt([P, S], U32, "hc%d" % b) for b in range(2)]
+        hs = [kt([P, S], U8, "hs%d" % b) for b in range(2)]
+        src = {}
+        for b in range(2):
+            for a in range(2):
+                src["w1%d%d" % (a, b)] = w1[512 * a:512 * (a + 1), 512 * b:512 * (b + 1)]
+            src["wg%d" % b] = wg[:, 512 * b:512 * (b + 1)]
+        for x in range(S // CTXW):
+            src["ctx%d" % x] = ctx[:, CTXW * x:CTXW * (x + 1)]
+        whole = {"wg": wg, "ctx": ctx, "w10": w1[0:512, :], "w11": w1[512:1024, :]}
+        rawfull = {k: kt([P, 4, 1024], F32, "raw" + k) for k in FULL}
+        raw = {k: (rawfull[k[:-1]][:, :, int(k[-1]) * src[k].shape[1]:(int(k[-1]) + 1) * src[k].shape[1]] if k[:-1] in FULL
+                   else kt([P, 4, src[k].shape[1]], F32, "raw" + k)) for k in src}
+        codes = {k: kt([P, src[k].shape[1]], U32, "codes" + k) for k in src}
+        scal = {k: kt([P, src[k].shape[1]], U8, "scal" + k) for k in src}
+        grouped, sig, pre, ads, hb = {}, {}, {}, {}, {}
+
+        def rows(tile, k, scales16):
+            for r in range(4):
+                if len(tile.shape) == 2:
+                    sq.dma_start(out=tile[k + r:P:32, :], in_=scales16[r:16:4, :].bitcast(I32))
+                else:
+                    sq.dma_start(out=tile[k + r:P:32, :, :], in_=scales16[r:16:4, :, :].bitcast(I32))
+
+        def load(name):
+            if name in FULL:
+                nc.sync.dma_start(out=rawfull[name][:], in_=whole[name].rearrange("(p i) c -> p i c", i=4))
+            elif name in src:
+                nc.sync.dma_start(out=raw[name][:], in_=src[name].rearrange("(p i) c -> p i c", i=4))
+            elif name == "list1":
+                nc.sync.dma_start(list1[:], offs)
+            elif name == "list2":
+                nc.sync.dma_start(list2[:], offs2)
+            elif name == "tab0" or name == "tab1":
+                a = int(name[3])
+                nc.sync.dma_start(out=tabw[a][:], in_=tab_words[a].rearrange("p t i -> p (t i)").bitcast(I32))
+            elif name == "tab2":
+                nc.sync.dma_start(out=tab2w[:], in_=tab2_words[0].rearrange("p t i -> p (t i)").bitcast(I32))
+            elif name == "w2":
+                nc.sync.dma_start(out=w2raw[:], in_=w2_words[0].bitcast(I32))
+            elif name == "wi":
+                nc.sync.dma_start(out=wiw[:], in_=wi_words.rearrange("a p e i -> p a (e i)").bitcast(I32))
+            elif name == "tabs":
+                nc.vector.memset(tabs[:], 0)
+                for q in range(4):
+                    sq.dma_start(out=tabs[32 * q + 4:32 * q + 12, :], in_=tab_scales[:, 4 * q:4 * q + 4, :].bitcast(I32))
+            elif name == "tab2s":
+                nc.vector.memset(tab2s[:], 0)
+                rows(tab2s[:], 0, tab2_scales[0])
+            elif name == "w2s":
+                nc.vector.memset(w2sraw[:], 0)
+                rows(w2sraw[:], 0, w2_scales[0])
+            elif name == "wis":
+                nc.vector.memset(wis[:], 0)
+                rows(wis[:], 12, wi_scales.rearrange("a q e -> q a e"))
+            elif name == "bias":
+                with nc.allow_non_contiguous_dma(reason="one bias value for each partition"):
+                    sq.dma_start(out=bias[:], in_=bi.rearrange("(c p) -> p c", p=P))
+
+        def cast(name, shares):
+            width = src[name].shape[1]
+            g = ring("grouped", GBUFS, [P, 2048], BF16)[:, 0:4 * width]
+            grouped[name] = g
+            if name.startswith("w"):
+                o = g[:].rearrange("p (t m i) -> p m i t", t=4, i=4)
+            else:
+                o = g[:].rearrange("p (m t i) -> p m i t", t=4, i=4)
+            i_ = raw[name][:].rearrange("p i (m t) -> p m i t", t=4)
+            sign = -1.0 if name.startswith("w1") else 1.0
+            m0 = 0
+            for e, m1 in shares:
+                m1 = m1 * width // 512
+                if e == "s":
+                    nc.scalar.activation(out=o[:, m0:m1], in_=i_[:, m0:m1], func=ACT.Copy, scale=sign)
+                elif e == "g":
+                    nc.gpsimd.tensor_scalar(o[:, m0:m1], i_[:, m0:m1], sign, 0.0, ALU.mult, ALU.add)
+                else:
+                    nc.vector.tensor_scalar(o[:, m0:m1], i_[:, m0:m1], sign, None, ALU.mult)
+                m0 = m1
+
+        def quant(name):
+            nc.vector.quantize_mx(out=codes[name][:].bitcast(FP8X4), scales=scal[name][:], in_=grouped[name][:])
+
+        def gather(which, jh):
+            cols = slice(32 * jh, 32 * jh + 32)
+            if which == "tabs":
+                nc.vector.tensor_copy(vs[jh][:], tabs[:].bitcast(U8).indirect(list1[:, cols]))
+            elif which == "tab2s":
+                nc.vector.tensor_copy(v2s[jh][:], tab2s[:].bitcast(U8).indirect(list2[:, cols]))
+            elif which == "tab2":
+                nc.vector.tensor_copy(v2w[jh][:], tab2w[:].bitcast(U32).indirect(list2[:, cols]))
+            else:
+                a = int(which[3])
+                nc.vector.tensor_copy(vw[a][jh][:], tabw[a][:].bitcast(U32).indirect(list1[:, cols]))
+
+        def perm():
+            nc.vector.tensor_copy(w2c[:].bitcast(U16).rearrange("p (b t m) -> p b t m", b=2, t=4),
+                                  w2raw[:].bitcast(U16).rearrange("p (b m t) -> p b t m", b=2, t=4))
+            nc.vector.tensor_copy(w2s[:].rearrange("p (b t m) -> p b t m", b=2, t=4),
+                                  w2sraw[:].bitcast(U8).rearrange("p (b m t) -> p b t m", b=2, t=4))
+
+        def mm(o, which, b, t, j0, n, start, stop):
+            jh, js = j0 // 512, slice(j0 % 512, j0 % 512 + n)
+            ms = slice(128 * t, 128 * t + 128)
+            if which == "d":
+                c0 = 512 * b + 128 * t
+                args = (w2c[:, 2 * c0:2 * c0 + 256].bitcast(FP4X4), w2s[:, c0:c0 + 128], v2w[jh][:, js].bitcast(FP8X4), v2s[jh][:, js])
+            elif which == "c":
+                x = "ctx%d" % (j0 // CTXW)
+                xs = slice(j0 % CTXW, j0 % CTXW + n)
+                args = (codes["wg%d" % b][:, ms].bitcast(FP8X4), scal["wg%d" % b][:, ms], codes[x][:, xs].bitcast(FP8X4), scal[x][:, xs])
+            else:
+                a = int(which[1])
+                w = "w1%d%d" % (a, b)
+                args = (codes[w][:, ms].bitcast(FP8X4), scal[w][:, ms], vw[a][jh][:, js].bitcast(FP8X4), vs[jh][4 + 4 * a:P, js])
+            nc.tensor.matmul_mx(out=o, lhsT=args[0], lhsT_scale=args[1], rhs=args[2], rhs_scale=args[3], start=start, stop=stop)
+
+        def cdir(b, q):
+            bk = bank("c")
+            for t in range(4):
+                mm(bk[:, 128 * t:128 * t + 128], "c", b, t, 128 * q, 128, True, True)
+            sg = ring("sig", SIGBUFS, [P, 128, 4], F32)
+            sig[b, q] = sg
+            nc.scalar.activation(out=sg[:], in_=bk[:].rearrange("p (t j) -> p j t", t=4), func=ACT.Sigmoid)
+            free_banks.append(bk)
+
+        def admm(b, q):
+            bk = bank("ad")
+            pre[b, q] = bk
+            for t in range(4):
+                for n_, which in enumerate(("d", "a0", "a1")):
+                    mm(bk[:, 128 * t:128 * t + 128], which, b, t, 128 * q, 128, n_ == 0, n_ == 2)
+
+        def addir(b, q):
+            bk = pre[b, q]
+            h = ring("hb", HBUFS, [P, 128, 4], BF16)
+            hb[b, q] = h
+            nc.vector.scalar_tensor_tensor(h[:], bk[:].rearrange("p (t j) -> p j t", t=4), -1.0, sig[b, q][:], ALU.mult, ALU.mult)
+            free_banks.append(bk)
+
+        def hq(b, q):
+            js = slice(128 * q, 128 * q + 128)
+            nc.vector.quantize_mx(out=hc[b][:, js].bitcast(FP8X4), scales=hs[b][:, js], in_=hb[b, q][:].rearrange("p j t -> p (j t)"))
+
+        def prepass(b, jh, which, start, stop):
+            for t in range(4):
+                if start:
+                    pre[b, jh, t] = bank("ad")
+                mm(pre[b, jh, t][:], which, b, t, 512 * jh, 512, start, stop)
+
+        def store(b, jh, engines):
+            ads[b, jh] = ring("ads", ABUFS, [P, 4, 512], F32)
+            for t in range(4):
+                if engines[t] == "s":
+                    nc.scalar.activation(out=ads[b, jh][:, t, :], in_=pre[b, jh, t][:], func=ACT.Copy, scale=-1.0)
+                else:
+                    nc.vector.tensor_scalar(ads[b, jh][:, t, :], pre[b, jh, t][:], -1.0, None, ALU.mult)
+                free_banks.append(pre[b, jh, t])
+
+        def hst(b, q, e):
+            h = ring("hb", HBUFS, [P, 128, 4], BF16)
+            hb[b, q] = h
+            j0 = 128 * q % 512
+            eng[e].tensor_tensor(h[:].rearrange("p (c x) t -> p c t x", x=4),
+                                 ads[b, q // 4][:, :, j0:j0 + 128].rearrange("p t (c x) -> p c t x", x=4),
+                                 sig[b, q][:].rearrange("p (c x) t -> p c t x", x=4), ALU.mult)
+
+        def cplan(b, jh, t):
+            bk = bank("c")
+            mm(bk[:], "c", b, t, 512 * jh, 512, True, True)
+            sg = ring("sig", SIGBUFS, [P, 128, 4], F32)
+            sig[b, jh, t] = sg
+            nc.scalar.activation(out=sg[:].rearrange("p j t -> p (j t)"), in_=bk[:], func=ACT.Sigmoid)
+            free_banks.append(bk)
+
+        def hplan(b, jh, t):
+            if t == 0:
+                ads[b, jh] = ring("hpl", 2, [P, 4, 512], BF16)
+            nc.vector.scalar_tensor_tensor(ads[b, jh][:, t, :], pre[b, jh, t][:], -1.0, sig[b, jh, t][:].rearrange("p j t -> p (j t)"),
+                                           ALU.mult, ALU.mult)
+            free_banks.append(pre[b, jh, t])
+
+        def inter(b, q, e):
+            h = ring("hb", HBUFS, [P, 128, 4], BF16)
+            hb[b, q] = h
+            j0 = 128 * q % 512
+            o = h[:].rearrange("p (c x) t -> p c t x", x=4)
+            i_ = ads[b, q // 4][:, :, j0:j0 + 128].rearrange("p t (c x) -> p c t x", x=4)
+            if e == "g":
+                nc.gpsimd.tensor_scalar(o, i_, 1.0, 0.0, ALU.mult, ALU.add)
+            elif e == "s":
+                nc.scalar.copy(o, i_)
+            else:
+                nc.vector.tensor_copy(o, i_)
+
+        def ystage(j0, n, engines, group):
+            js = slice(j0, j0 + n)
+            per_bank = group
+            for c0 in range(0, 6, group):
+                res = ring("res", YBUFS, [P, 512], F32)[:, 0:group * n].rearrange("p (c j) -> p c j", c=group)
+                for c in range(c0, c0 + group):
+                    if c % per_bank == 0:
+                        bk = bank("y")
+                    o = bk[:, (c % per_bank) * n:(c % per_bank + 1) * n]
+                    for b in range(2):
+                        nc.tensor.matmul_mx(out=o, lhsT=wiw[:, b, 128 * c:128 * c + 128].bitcast(FP8X4),
+                                            lhsT_scale=wis[12:P, b, :].bitcast(U8)[:, 128 * c:128 * c + 128],
+                                            rhs=hc[b][:, js].bitcast(FP8X4), rhs_scale=hs[b][:, js], start=b == 0, stop=b == 1)
+                    if engines[c] == "s":
+                        nc.scalar.activation(out=res[:, c - c0, :], in_=o, func=ACT.Identity, bias=bias[:, c:c + 1])
+                    else:
+                        nc.vector.tensor_scalar(res[:, c - c0, :], o, bias[:, c:c + 1], None, ALU.add)
+                    if c % per_bank == per_bank - 1:
+                        free_banks.append(bk)
+                nc.sync.dma_start(out=out.rearrange("(c p) j -> p c j", p=P)[:, c0:c0 + group, js], in_=res[:])
+
+        fns = dict(load=load, cast=cast, quant=quant, gather=gather, perm=perm, c=cdir, ad=addir, hq=hq, pre=prepass, store=store,
+                   hst=hst, y=ystage, adm=admm, cp=cplan, hp=hplan, il=inter)
+        for step in PLAN:
+            fns[step[0]](*step[1:])

@@ -9,121 +9,136 @@ I32, U32, U16, U8 = mybir.dt.int32, mybir.dt.uint32, mybir.dt.uint16, mybir.dt.u
 FP8X4, FP4X4 = mybir.dt.float8_e4m3fn_x4, mybir.dt.float4_e2m1fn_x4
 ACT, ALU = mybir.ActivationFunctionType, mybir.AluOpType
 P = 128
-SCALEQ = "gpsimd"
+SCALEQ = "sync"
 PLAN = [
     ('load', 'list2'),
     ('load', 'list1'),
-    ('load', 'tab2s'),
-    ('load', 'w2s'),
+    ('load', 'tab2s0'),
+    ('load', 'tab2s1'),
     ('load', 'bias'),
-    ('load', 'tabs'),
-    ('load', 'wis'),
-    ('load', 'w110'),
-    ('load', 'w2'),
-    ('load', 'tab2'),
-    ('load', 'tab0'),
+    ('load', 'w2s1'),
+    ('load', 'tab2s3'),
     ('load', 'w10'),
+    ('load', 'w2'),
+    ('load', 'tabs7'),
+    ('load', 'tab2'),
+    ('load', 'tab2s2'),
+    ('load', 'w110'),
+    ('load', 'tabs0'),
+    ('load', 'w2s0'),
+    ('load', 'wis0'),
+    ('load', 'tabs1'),
+    ('load', 'w2s3'),
+    ('load', 'tab0'),
+    ('load', 'tabs2'),
+    ('load', 'tabs5'),
+    ('load', 'tabs3'),
+    ('load', 'w2s2'),
+    ('load', 'tabs6'),
+    ('load', 'tabs4'),
     ('load', 'tab1'),
     ('load', 'wg0'),
+    ('load', 'wis2'),
     ('load', 'ctx0'),
-    ('load', 'w111'),
     ('load', 'wg1'),
+    ('load', 'w111'),
+    ('load', 'wis1'),
+    ('load', 'wis3'),
     ('load', 'ctx1'),
     ('load', 'wi'),
     ('gather', 'tabs', 1),
-    ('gather', 'tab2s', 0),
-    ('cast', 'w110', [('s', 80), ('v', 128)]),
-    ('quant', 'w110'),
-    ('gather', 'tab2s', 1),
-    ('gather', 'tab0', 1),
-    ('gather', 'tab2', 0),
     ('cast', 'w100', [('s', 64), ('v', 128)]),
-    ('cast', 'w101', [('s', 96), ('v', 128)]),
-    ('quant', 'w100'),
-    ('pre', 0, 1, 'a0', True, False),
-    ('perm',),
-    ('gather', 'tab2', 1),
+    ('gather', 'tab0', 1),
+    ('cast', 'w101', [('s', 64), ('v', 128)]),
     ('gather', 'tab0', 0),
+    ('cast', 'w110', [('s', 64), ('v', 128)]),
+    ('quant', 'w100'),
+    ('quant', 'w110'),
     ('quant', 'w101'),
-    ('gather', 'tabs', 0),
-    ('pre', 0, 1, 'd', False, False),
-    ('cast', 'ctx0', [('s', 64), ('v', 128)]),
-    ('cast', 'w111', [('s', 48), ('v', 128)]),
-    ('cast', 'wg0', [('s', 80), ('v', 128)]),
-    ('quant', 'wg0'),
-    ('gather', 'tab1', 1),
-    ('pre', 0, 1, 'a1', False, True),
-    ('store', 0, 1, 'svsv'),
-    ('quant', 'ctx0'),
-    ('c', 0, 0),
-    ('c', 0, 3),
-    ('c', 0, 2),
-    ('gather', 'tab1', 0),
-    ('pre', 0, 0, 'a1', True, False),
-    ('pre', 0, 0, 'a0', False, False),
-    ('cast', 'ctx1', [('s', 48), ('v', 128)]),
-    ('quant', 'w111'),
-    ('adm', 1, 2),
-    ('adm', 1, 3),
-    ('adm', 1, 4),
-    ('pre', 0, 0, 'd', False, True),
-    ('store', 0, 0, 'svsv'),
-    ('hst', 0, 0, 'v'),
-    ('hst', 0, 3, 'v'),
-    ('hst', 0, 2, 'v'),
-    ('adm', 1, 1),
-    ('cast', 'wg1', [('s', 80), ('v', 128)]),
+    ('cast', 'wg1', [('v', 128)]),
     ('quant', 'wg1'),
+    ('gather', 'tab1', 0),
+    ('gather', 'tab1', 1),
+    ('cast', 'wg0', [('s', 64), ('v', 128)]),
+    ('quant', 'wg0'),
+    ('gather', 'tab2', 0),
+    ('cast', 'ctx0', [('s', 32), ('v', 128)]),
+    ('perm',),
+    ('gather', 'tabs', 0),
+    ('pre', 0, 0, 'a0', True, False),
+    ('pre', 0, 0, 'a1', False, False),
+    ('gather', 'tab2', 1),
+    ('gather', 'tab2s', 0),
+    ('pre', 0, 0, 'd', False, True),
+    ('gather', 'tab2s', 1),
+    ('pre', 0, 1, 'd', True, False),
+    ('pre', 0, 1, 'a1', False, False),
+    ('pre', 0, 1, 'a0', False, True),
+    ('store', 0, 1, 'ssss'),
+    ('store', 0, 0, 'svsv'),
+    ('cast', 'w111', [('s', 64), ('v', 128)]),
+    ('cast', 'ctx1', [('s', 80), ('v', 128)]),
+    ('quant', 'ctx0'),
+    ('c', 0, 3),
+    ('c', 0, 0),
     ('c', 1, 0),
+    ('c', 0, 2),
+    ('hst', 0, 2, 'v'),
+    ('hst', 0, 0, 'v'),
     ('c', 0, 1),
-    ('hst', 0, 1, 'v'),
-    ('c', 1, 1),
-    ('adm', 1, 5),
+    ('hst', 0, 3, 'v'),
     ('c', 1, 2),
     ('c', 1, 3),
+    ('c', 1, 1),
+    ('hst', 0, 1, 'v'),
+    ('quant', 'w111'),
+    ('adm', 1, 2),
+    ('adm', 1, 4),
+    ('adm', 1, 3),
     ('adm', 1, 0),
-    ('quant', 'ctx1'),
-    ('c', 0, 6),
-    ('c', 0, 5),
+    ('adm', 1, 1),
+    ('adm', 1, 5),
     ('hq', 0, 3),
+    ('quant', 'ctx1'),
+    ('c', 0, 5),
+    ('c', 0, 7),
+    ('adm', 1, 6),
     ('hq', 0, 0),
+    ('hq', 0, 1),
+    ('hq', 0, 2),
     ('ad', 1, 1),
     ('ad', 1, 0),
-    ('hq', 0, 2),
     ('ad', 1, 3),
-    ('c', 0, 7),
-    ('hq', 0, 1),
+    ('c', 0, 6),
+    ('hq', 1, 0),
     ('ad', 1, 2),
-    ('adm', 1, 6),
     ('c', 0, 4),
     ('hq', 1, 1),
     ('hst', 0, 4, 'v'),
-    ('c', 1, 7),
     ('hq', 1, 3),
     ('c', 1, 6),
-    ('hq', 1, 0),
     ('ad', 1, 6),
     ('hst', 0, 5, 'v'),
+    ('c', 1, 4),
+    ('c', 1, 7),
     ('c', 1, 5),
     ('adm', 1, 7),
-    ('c', 1, 4),
+    ('hq', 0, 4),
     ('hq', 1, 2),
     ('ad', 1, 4),
-    ('y', 0, 512, 'ssvvss', 1),
-    ('hq', 0, 4),
+    ('y', 0, 512, 'ssssss', 1),
     ('ad', 1, 5),
     ('hq', 1, 5),
-    ('hq', 0, 5),
     ('hq', 1, 4),
-    ('y', 512, 256, 'ssssvv', 2),
     ('hq', 1, 6),
     ('ad', 1, 7),
-    ('hst', 0, 7, 'v'),
+    ('hq', 0, 5),
     ('hst', 0, 6, 'v'),
+    ('hst', 0, 7, 'v'),
+    ('hq', 0, 7),
     ('hq', 0, 6),
     ('hq', 1, 7),
-    ('hq', 0, 7),
-    ('y', 768, 256, 'sssvvv', 2),
+    ('y', 512, 512, 'svsvsv', 1),
 ]
 SIGBUFS = 8
 PSB = {"c": 2, "ad": 3, "y": 3}
@@ -194,12 +209,10 @@ def tile_list_session_shift_recommender_kernel(tc, tab_words, tab_scales, offs, 
         scal = {k: kt([P, src[k].shape[1]], U8, "scal" + k) for k in src}
         grouped, sig, pre, ads, hb = {}, {}, {}, {}, {}
 
-        def rows(tile, k, scales16):
-            for r in range(4):
-                if len(tile.shape) == 2:
-                    sq.dma_start(out=tile[k + r:P:32, :], in_=scales16[r:16:4, :].bitcast(I32))
-                else:
-                    sq.dma_start(out=tile[k + r:P:32, :, :], in_=scales16[r:16:4, :, :].bitcast(I32))
+        nc.vector.memset(tab2s[:], 0)
+        nc.gpsimd.memset(w2sraw[:], 0)
+        nc.vector.memset(tabs[:], 0)
+        nc.gpsimd.memset(wis[:], 0)
 
         def load(name):
             if name in FULL:
@@ -219,19 +232,18 @@ def tile_list_session_shift_recommender_kernel(tc, tab_words, tab_scales, offs, 
                 nc.sync.dma_start(out=w2raw[:], in_=w2_words[0].bitcast(I32))
             elif name == "wi":
                 nc.sync.dma_start(out=wiw[:], in_=wi_words.rearrange("a p e i -> p a (e i)").bitcast(I32))
-            elif name == "tabs":
-                nc.vector.memset(tabs[:], 0)
-                for q in range(4):
-                    sq.dma_start(out=tabs[32 * q + 4:32 * q + 12, :], in_=tab_scales[:, 4 * q:4 * q + 4, :].bitcast(I32))
-            elif name == "tab2s":
-                nc.vector.memset(tab2s[:], 0)
-                rows(tab2s[:], 0, tab2_scales[0])
-            elif name == "w2s":
-                nc.vector.memset(w2sraw[:], 0)
-                rows(w2sraw[:], 0, w2_scales[0])
-            elif name == "wis":
-                nc.vector.memset(wis[:], 0)
-                rows(wis[:], 12, wi_scales.rearrange("a q e -> q a e"))
+            elif name.startswith("tabs"):
+                a, r = divmod(int(name[4]), 4)
+                sq.dma_start(out=tabs[4 + 4 * a + r:P:32, :], in_=tab_scales[a, r:16:4, :].bitcast(I32))
+            elif name.startswith("tab2s"):
+                r = int(name[5])
+                sq.dma_start(out=tab2s[r:P:32, :], in_=tab2_scales[0, r:16:4, :].bitcast(I32))
+            elif name.startswith("w2s"):
+                r = int(name[3])
+                sq.dma_start(out=w2sraw[r:P:32, :], in_=w2_scales[0, r:16:4, :].bitcast(I32))
+            elif name.startswith("wis"):
+                r = int(name[3])
+                sq.dma_start(out=wis[12 + r:P:32, :, :], in_=wi_scales.rearrange("a q e -> q a e")[r:16:4, :, :].bitcast(I32))
             elif name == "bias":
                 with nc.allow_non_contiguous_dma(reason="one bias value for each partition"):
                     sq.dma_start(out=bias[:], in_=bi.rearrange("(c p) -> p c", p=P))
@@ -248,13 +260,16 @@ def tile_list_session_shift_recommender_kernel(tc, tab_words, tab_scales, offs, 
             sign = -1.0 if name.startswith("w1") else 1.0
             m0 = 0
             for e, m1 in shares:
-                m1 = m1 * width // 512
-                if e == "s":
-                    nc.scalar.activation(out=o[:, m0:m1], in_=i_[:, m0:m1], func=ACT.Copy, scale=sign)
-                elif e == "g":
-                    nc.gpsimd.tensor_scalar(o[:, m0:m1], i_[:, m0:m1], sign, 0.0, ALU.mult, ALU.add)
+                if name.startswith("w"):
+                    oo, ii = o[:, :, :, m0 // 32:m1 // 32], i_[:, :, :, m0 // 32:m1 // 32]
                 else:
-                    nc.vector.tensor_scalar(o[:, m0:m1], i_[:, m0:m1], sign, None, ALU.mult)
+                    oo, ii = o[:, m0 * width // 512:m1 * width // 512], i_[:, m0 * width // 512:m1 * width // 512]
+                if e == "s":
+                    nc.scalar.activation(out=oo, in_=ii, func=ACT.Copy, scale=sign)
+                elif e == "g":
+                    nc.gpsimd.tensor_scalar(oo, ii, sign, 0.0, ALU.mult, ALU.add)
+                else:
+                    nc.vector.tensor_scalar(oo, ii, sign, None, ALU.mult)
                 m0 = m1
 
         def quant(name):

@@ -1,6 +1,7 @@
 from contextlib import ExitStack
 
 import concourse.mybir as mybir
+from concourse.masks import make_identity
 
 K, K2, C, H, N, T, T2, S = 1024, 512, 512, 1024, 768, 4096, 2048, 1024
 FLOPS = 2 * S * (K * H + K2 * H + C * H + H * N)
@@ -9,146 +10,154 @@ I32, U32, U16, U8 = mybir.dt.int32, mybir.dt.uint32, mybir.dt.uint16, mybir.dt.u
 FP8X4, FP4X4 = mybir.dt.float8_e4m3fn_x4, mybir.dt.float4_e2m1fn_x4
 ACT, ALU = mybir.ActivationFunctionType, mybir.AluOpType
 P = 128
-SCALEQ = "sync"
+SCALEQ = 'sync'
 PLAN = [
     ('load', 'list2'),
     ('load', 'list1'),
-    ('load', 'tab2s0'),
-    ('load', 'tab2s1'),
-    ('load', 'bias'),
+    ('load', 'tabs7'),
+    ('load', 'tabs6'),
+    ('load', 'w2s0'),
+    ('load', 'tabs4'),
+    ('load', 'wg'),
+    ('load', 'w2s2'),
+    ('load', 'tabs3'),
+    ('load', 'w2'),
+    ('load', 'tabs0'),
+    ('load', 'ctx'),
+    ('load', 'tabs2'),
+    ('load', 'w2s3'),
+    ('load', 'w110'),
     ('load', 'w2s1'),
     ('load', 'tab2s3'),
-    ('load', 'w10'),
-    ('load', 'w2'),
-    ('load', 'tabs7'),
     ('load', 'tab2'),
-    ('load', 'tab2s2'),
-    ('load', 'w110'),
-    ('load', 'tabs0'),
-    ('load', 'w2s0'),
-    ('load', 'wis0'),
+    ('load', 'tab2s1'),
+    ('load', 'tab2s0'),
     ('load', 'tabs1'),
-    ('load', 'w2s3'),
-    ('load', 'tab0'),
-    ('load', 'tabs2'),
-    ('load', 'tabs5'),
-    ('load', 'tabs3'),
-    ('load', 'w2s2'),
-    ('load', 'tabs6'),
-    ('load', 'tabs4'),
+    ('load', 'tab2s2'),
+    ('load', 'w100'),
     ('load', 'tab1'),
-    ('load', 'wg0'),
-    ('load', 'wis2'),
-    ('load', 'ctx0'),
-    ('load', 'wg1'),
+    ('load', 'tab0'),
     ('load', 'w111'),
-    ('load', 'wis1'),
+    ('load', 'w101'),
+    ('load', 'wis2'),
+    ('load', 'bias'),
     ('load', 'wis3'),
-    ('load', 'ctx1'),
+    ('load', 'wis0'),
     ('load', 'wi'),
-    ('gather', 'tabs', 1),
-    ('cast', 'w100', [('s', 64), ('v', 128)]),
-    ('gather', 'tab0', 1),
-    ('cast', 'w101', [('s', 64), ('v', 128)]),
-    ('gather', 'tab0', 0),
+    ('load', 'wis1'),
+    ('load', 'tabs5'),
+    ('cast', 'ctx0', [('s', 32), ('v', 128)]),
+    ('quant', 'ctx0'),
+    ('cast', 'wg1', [('s', 128)]),
     ('cast', 'w110', [('s', 64), ('v', 128)]),
-    ('quant', 'w100'),
     ('quant', 'w110'),
-    ('quant', 'w101'),
-    ('cast', 'wg1', [('v', 128)]),
+    ('gather', 'tab2s', 0),
     ('quant', 'wg1'),
-    ('gather', 'tab1', 0),
-    ('gather', 'tab1', 1),
+    ('gather', 'tabs', 1),
     ('cast', 'wg0', [('s', 64), ('v', 128)]),
     ('quant', 'wg0'),
-    ('gather', 'tab2', 0),
-    ('cast', 'ctx0', [('s', 32), ('v', 128)]),
-    ('perm',),
-    ('gather', 'tabs', 0),
-    ('pre', 0, 0, 'a0', True, False),
-    ('pre', 0, 0, 'a1', False, False),
-    ('gather', 'tab2', 1),
-    ('gather', 'tab2s', 0),
-    ('pre', 0, 0, 'd', False, True),
-    ('gather', 'tab2s', 1),
-    ('pre', 0, 1, 'd', True, False),
-    ('pre', 0, 1, 'a1', False, False),
-    ('pre', 0, 1, 'a0', False, True),
-    ('store', 0, 1, 'ssss'),
-    ('store', 0, 0, 'svsv'),
-    ('cast', 'w111', [('s', 64), ('v', 128)]),
-    ('cast', 'ctx1', [('s', 80), ('v', 128)]),
-    ('quant', 'ctx0'),
-    ('c', 0, 3),
-    ('c', 0, 0),
-    ('c', 1, 0),
-    ('c', 0, 2),
-    ('hst', 0, 2, 'v'),
-    ('hst', 0, 0, 'v'),
     ('c', 0, 1),
-    ('hst', 0, 3, 'v'),
-    ('c', 1, 2),
+    ('cast', 'ctx1', [('s', 112), ('v', 128)]),
+    ('gather', 'tabs', 0),
+    ('gather', 'tab1', 0),
     ('c', 1, 3),
-    ('c', 1, 1),
-    ('hst', 0, 1, 'v'),
+    ('gather', 'tab1', 1),
+    ('quant', 'ctx1'),
+    ('gather', 'tab2s', 1),
+    ('gather', 'tab0', 1),
+    ('gather', 'tab2', 0),
+    ('cast', 'w100', [('v', 128)]),
+    ('quant', 'w100'),
+    ('gather', 'tab2', 1),
+    ('c', 0, 2),
+    ('perm',),
+    ('c', 0, 0),
+    ('cp', 0, 1, 1),
+    ('cp', 1, 1, 1),
+    ('cp', 0, 1, 3),
+    ('cp', 0, 1, 2),
+    ('c', 1, 2),
+    ('cp', 0, 1, 0),
+    ('cast', 'w111', [('s', 128)]),
     ('quant', 'w111'),
-    ('adm', 1, 2),
-    ('adm', 1, 4),
-    ('adm', 1, 3),
+    ('cp', 1, 1, 0),
+    ('c', 0, 3),
+    ('gather', 'tab0', 0),
+    ('adm', 0, 0),
+    ('cp', 1, 1, 3),
+    ('ad', 0, 0),
+    ('pre', 0, 1, 'a1', True, False),
+    ('cast', 'w101', [('s', 128)]),
+    ('quant', 'w101'),
+    ('cp', 1, 1, 2),
+    ('pre', 0, 1, 'd', False, False),
+    ('pre', 0, 1, 'a0', False, True),
+    ('c', 1, 1),
+    ('pre', 1, 1, 'd', True, False),
+    ('hp', 0, 1, 0),
+    ('pre', 1, 1, 'a1', False, False),
+    ('hq', 0, 0),
+    ('hp', 0, 1, 1),
+    ('adm', 0, 2),
+    ('ad', 0, 2),
+    ('adm', 0, 1),
+    ('ad', 0, 1),
+    ('hp', 0, 1, 2),
+    ('biast',),
+    ('adm', 0, 3),
+    ('pre', 1, 1, 'a0', False, True),
+    ('c', 1, 0),
+    ('hp', 0, 1, 3),
+    ('hp', 1, 1, 0),
+    ('hq', 0, 1),
+    ('il', 0, 6, 'v'),
+    ('hq', 0, 2),
+    ('il', 0, 7, 's'),
+    ('il', 0, 5, 's'),
+    ('hp', 1, 1, 1),
+    ('hp', 1, 1, 2),
+    ('hp', 1, 1, 3),
+    ('hq', 0, 6),
+    ('il', 0, 4, 's'),
+    ('hq', 0, 5),
+    ('hq', 0, 7),
+    ('il', 1, 6, 's'),
+    ('il', 1, 5, 'v'),
+    ('hq', 0, 4),
+    ('il', 1, 7, 'v'),
+    ('il', 1, 4, 's'),
     ('adm', 1, 0),
     ('adm', 1, 1),
-    ('adm', 1, 5),
-    ('hq', 0, 3),
-    ('quant', 'ctx1'),
-    ('c', 0, 5),
-    ('c', 0, 7),
-    ('adm', 1, 6),
-    ('hq', 0, 0),
-    ('hq', 0, 1),
-    ('hq', 0, 2),
-    ('ad', 1, 1),
-    ('ad', 1, 0),
-    ('ad', 1, 3),
-    ('c', 0, 6),
-    ('hq', 1, 0),
-    ('ad', 1, 2),
-    ('c', 0, 4),
-    ('hq', 1, 1),
-    ('hst', 0, 4, 'v'),
-    ('hq', 1, 3),
-    ('c', 1, 6),
-    ('ad', 1, 6),
-    ('hst', 0, 5, 'v'),
-    ('c', 1, 4),
-    ('c', 1, 7),
-    ('c', 1, 5),
-    ('adm', 1, 7),
-    ('hq', 0, 4),
-    ('hq', 1, 2),
-    ('ad', 1, 4),
-    ('y', 0, 512, 'ssssss', 1),
-    ('ad', 1, 5),
     ('hq', 1, 5),
-    ('hq', 1, 4),
-    ('hq', 1, 6),
-    ('ad', 1, 7),
-    ('hq', 0, 5),
-    ('hst', 0, 6, 'v'),
-    ('hst', 0, 7, 'v'),
-    ('hq', 0, 7),
-    ('hq', 0, 6),
     ('hq', 1, 7),
-    ('y', 512, 512, 'svsvsv', 1),
+    ('hq', 1, 6),
+    ('adm', 1, 2),
+    ('adm', 1, 3),
+    ('hq', 1, 4),
+    ('ad', 0, 3),
+    ('y', 512, 512, 'ssssss', 1),
+    ('hq', 0, 3),
+    ('ad', 1, 3),
+    ('ad', 1, 0),
+    ('ad', 1, 2),
+    ('ad', 1, 1),
+    ('hq', 1, 0),
+    ('hq', 1, 1),
+    ('hq', 1, 3),
+    ('hq', 1, 2),
+    ('y', 0, 512, 'vvsvss', 1),
 ]
-SIGBUFS = 8
+SIGBUFS = 15
 PSB = {"c": 2, "ad": 3, "y": 3}
 ONEPOOL = False
 YBUFS = 6
 CTXW = 512
+ALIAS = True
+QFORM = True
 GBUFS = 3
 HBUFS = 4
-ABUFS = 2
-FULL = ('w10',)
+ABUFS = 3
+FULL = ('wg', 'ctx')
 
 
 def tile_list_session_shift_recommender_kernel(tc, tab_words, tab_scales, offs, tab2_words, tab2_scales, offs2, ctx, w1,
@@ -207,12 +216,32 @@ def tile_list_session_shift_recommender_kernel(tc, tab_words, tab_scales, offs, 
                    else kt([P, 4, src[k].shape[1]], F32, "raw" + k)) for k in src}
         codes = {k: kt([P, src[k].shape[1]], U32, "codes" + k) for k in src}
         scal = {k: kt([P, src[k].shape[1]], U8, "scal" + k) for k in src}
+        spent = {}
+        for k in ("wg", "ctx"):
+            if k in FULL:
+                flat = rawfull[k][:].rearrange("p i c -> p (i c)")
+                spent[k] = [flat[:, 0:2048], flat[:, 2048:4096]]
+            else:
+                spent[k] = [raw[k + x][:].rearrange("p i c -> p (i c)") for x in "01"]
+        if ALIAS:
+            rings["ads"] = [x.rearrange("p (t j) -> p t j", t=4) for x in spent["wg"]] + [kt([P, 4, 512], F32, "ads2")[:]]
+        rings["res"] = [x[:, 512 * u:512 * u + 512] for x in spent["ctx"] for u in range(4)]
         grouped, sig, pre, ads, hb = {}, {}, {}, {}, {}
 
         nc.vector.memset(tab2s[:], 0)
         nc.gpsimd.memset(w2sraw[:], 0)
         nc.vector.memset(tabs[:], 0)
         nc.gpsimd.memset(wis[:], 0)
+        brows = kt([P, P], F32, "brows")
+        ident = kt([P, P], F32, "ident")
+        nc.gpsimd.memset(brows[:], 0.0)
+        make_identity(nc, ident[:])
+
+        def biast():
+            bk = bank("b")
+            nc.tensor.transpose(bk[:, 0:P], brows[:], ident[:])
+            nc.scalar.copy(bias[:], bk[:, 0:N // P])
+            free_banks.append(bk)
 
         def load(name):
             if name in FULL:
@@ -234,19 +263,23 @@ def tile_list_session_shift_recommender_kernel(tc, tab_words, tab_scales, offs, 
                 nc.sync.dma_start(out=wiw[:], in_=wi_words.rearrange("a p e i -> p a (e i)").bitcast(I32))
             elif name.startswith("tabs"):
                 a, r = divmod(int(name[4]), 4)
-                sq.dma_start(out=tabs[4 + 4 * a + r:P:32, :], in_=tab_scales[a, r:16:4, :].bitcast(I32))
+                if not QFORM:
+                    sq.dma_start(out=tabs[4 + 4 * a + r:P:32, :], in_=tab_scales[a, r:16:4, :].bitcast(I32))
+                elif a == 0:
+                    sq.dma_start(out=tabs[32 * r + 4:32 * r + 12, :], in_=tab_scales[:, 4 * r:4 * r + 4, :].bitcast(I32))
             elif name.startswith("tab2s"):
                 r = int(name[5])
                 sq.dma_start(out=tab2s[r:P:32, :], in_=tab2_scales[0, r:16:4, :].bitcast(I32))
             elif name.startswith("w2s"):
                 r = int(name[3])
-                sq.dma_start(out=w2sraw[r:P:32, :], in_=w2_scales[0, r:16:4, :].bitcast(I32))
+                nc.sync.dma_start(out=w2sraw[r:P:32, :], in_=w2_scales[0, r:16:4, :].bitcast(I32))
             elif name.startswith("wis"):
                 r = int(name[3])
-                sq.dma_start(out=wis[12 + r:P:32, :, :], in_=wi_scales.rearrange("a q e -> q a e")[r:16:4, :, :].bitcast(I32))
+                nc.sync.dma_start(out=wis[12 + r:P:32, :, :], in_=wi_scales.rearrange("a q e -> q a e")[r:16:4, :, :].bitcast(I32))
             elif name == "bias":
-                with nc.allow_non_contiguous_dma(reason="one bias value for each partition"):
-                    sq.dma_start(out=bias[:], in_=bi.rearrange("(c p) -> p c", p=P))
+                rows6 = bi.rearrange("(c p) -> c p", p=P)
+                nc.sync.dma_start(out=brows[0:4, :], in_=rows6[0:4, :])
+                nc.sync.dma_start(out=brows[4:6, :], in_=rows6[4:6, :])
 
         def cast(name, shares):
             width = src[name].shape[1]
@@ -409,6 +442,6 @@ def tile_list_session_shift_recommender_kernel(tc, tab_words, tab_scales, offs, 
                 nc.sync.dma_start(out=out.rearrange("(c p) j -> p c j", p=P)[:, c0:c0 + group, js], in_=res[:])
 
         fns = dict(load=load, cast=cast, quant=quant, gather=gather, perm=perm, c=cdir, ad=addir, hq=hq, pre=prepass, store=store,
-                   hst=hst, y=ystage, adm=admm, cp=cplan, hp=hplan, il=inter)
+                   hst=hst, y=ystage, biast=biast, adm=admm, cp=cplan, hp=hplan, il=inter)
         for step in PLAN:
             fns[step[0]](*step[1:])

@@ -5,443 +5,357 @@ from concourse.masks import make_identity
 
 K, K2, C, H, N, T, T2, S = 1024, 512, 512, 1024, 768, 4096, 2048, 1024
 FLOPS = 2 * S * (K * H + K2 * H + C * H + H * N)
+
 F32, BF16 = mybir.dt.float32, mybir.dt.bfloat16
 I32, U32, U16, U8 = mybir.dt.int32, mybir.dt.uint32, mybir.dt.uint16, mybir.dt.uint8
 FP8X4, FP4X4 = mybir.dt.float8_e4m3fn_x4, mybir.dt.float4_e2m1fn_x4
 ACT, ALU = mybir.ActivationFunctionType, mybir.AluOpType
+
 P = 128
-SCALEQ = 'sync'
-PLAN = [
-    ('load', 'list2'),
-    ('load', 'list1'),
-    ('load', 'tabs7'),
-    ('load', 'tabs6'),
-    ('load', 'w2s0'),
-    ('load', 'tabs4'),
-    ('load', 'wg'),
-    ('load', 'w2s2'),
-    ('load', 'tabs3'),
-    ('load', 'w2'),
-    ('load', 'tabs0'),
-    ('load', 'ctx'),
-    ('load', 'tabs2'),
-    ('load', 'w2s3'),
-    ('load', 'w110'),
-    ('load', 'w2s1'),
-    ('load', 'tab2s3'),
-    ('load', 'tab2'),
-    ('load', 'tab2s1'),
-    ('load', 'tab2s0'),
-    ('load', 'tabs1'),
-    ('load', 'tab2s2'),
-    ('load', 'w100'),
-    ('load', 'tab1'),
-    ('load', 'tab0'),
-    ('load', 'w111'),
-    ('load', 'w101'),
-    ('load', 'wis2'),
-    ('load', 'bias'),
-    ('load', 'wis3'),
-    ('load', 'wis0'),
-    ('load', 'wi'),
-    ('load', 'wis1'),
-    ('load', 'tabs5'),
-    ('cast', 'ctx0', [('s', 32), ('v', 128)]),
-    ('quant', 'ctx0'),
-    ('cast', 'wg1', [('s', 128)]),
-    ('cast', 'w110', [('s', 64), ('v', 128)]),
-    ('quant', 'w110'),
-    ('gather', 'tab2s', 0),
-    ('quant', 'wg1'),
-    ('gather', 'tabs', 1),
-    ('cast', 'wg0', [('s', 64), ('v', 128)]),
-    ('quant', 'wg0'),
-    ('c', 0, 1),
-    ('cast', 'ctx1', [('s', 112), ('v', 128)]),
-    ('gather', 'tabs', 0),
-    ('gather', 'tab1', 0),
-    ('c', 1, 3),
-    ('gather', 'tab1', 1),
-    ('quant', 'ctx1'),
-    ('gather', 'tab2s', 1),
-    ('gather', 'tab0', 1),
-    ('gather', 'tab2', 0),
-    ('cast', 'w100', [('v', 128)]),
-    ('quant', 'w100'),
-    ('gather', 'tab2', 1),
-    ('c', 0, 2),
-    ('perm',),
-    ('c', 0, 0),
-    ('cp', 0, 1, 1),
-    ('cp', 1, 1, 1),
-    ('cp', 0, 1, 3),
-    ('cp', 0, 1, 2),
-    ('c', 1, 2),
-    ('cp', 0, 1, 0),
-    ('cast', 'w111', [('s', 128)]),
-    ('quant', 'w111'),
-    ('cp', 1, 1, 0),
-    ('c', 0, 3),
-    ('gather', 'tab0', 0),
-    ('adm', 0, 0),
-    ('cp', 1, 1, 3),
-    ('ad', 0, 0),
-    ('pre', 0, 1, 'a1', True, False),
-    ('cast', 'w101', [('s', 128)]),
-    ('quant', 'w101'),
-    ('cp', 1, 1, 2),
-    ('pre', 0, 1, 'd', False, False),
-    ('pre', 0, 1, 'a0', False, True),
-    ('c', 1, 1),
-    ('pre', 1, 1, 'd', True, False),
-    ('hp', 0, 1, 0),
-    ('pre', 1, 1, 'a1', False, False),
-    ('hq', 0, 0),
-    ('hp', 0, 1, 1),
-    ('adm', 0, 2),
-    ('ad', 0, 2),
-    ('adm', 0, 1),
-    ('ad', 0, 1),
-    ('hp', 0, 1, 2),
-    ('biast',),
-    ('adm', 0, 3),
-    ('pre', 1, 1, 'a0', False, True),
-    ('c', 1, 0),
-    ('hp', 0, 1, 3),
-    ('hp', 1, 1, 0),
-    ('hq', 0, 1),
-    ('il', 0, 6, 'v'),
-    ('hq', 0, 2),
-    ('il', 0, 7, 's'),
-    ('il', 0, 5, 's'),
-    ('hp', 1, 1, 1),
-    ('hp', 1, 1, 2),
-    ('hp', 1, 1, 3),
-    ('hq', 0, 6),
-    ('il', 0, 4, 's'),
-    ('hq', 0, 5),
-    ('hq', 0, 7),
-    ('il', 1, 6, 's'),
-    ('il', 1, 5, 'v'),
-    ('hq', 0, 4),
-    ('il', 1, 7, 'v'),
-    ('il', 1, 4, 's'),
-    ('adm', 1, 0),
-    ('adm', 1, 1),
-    ('hq', 1, 5),
-    ('hq', 1, 7),
-    ('hq', 1, 6),
-    ('adm', 1, 2),
-    ('adm', 1, 3),
-    ('hq', 1, 4),
-    ('ad', 0, 3),
-    ('y', 512, 512, 'ssssss', 1),
-    ('hq', 0, 3),
-    ('ad', 1, 3),
-    ('ad', 1, 0),
-    ('ad', 1, 2),
-    ('ad', 1, 1),
-    ('hq', 1, 0),
-    ('hq', 1, 1),
-    ('hq', 1, 3),
-    ('hq', 1, 2),
-    ('y', 0, 512, 'vvsvss', 1),
-]
-SIGBUFS = 15
-PSB = {"c": 2, "ad": 3, "y": 3}
-ONEPOOL = False
-YBUFS = 6
-CTXW = 512
-ALIAS = True
-QFORM = True
-GBUFS = 3
-HBUFS = 4
-ABUFS = 3
-FULL = ('wg', 'ctx')
+PACK = 4
+PASS = P * PACK
+WIDE = 512
+NARROW = 128
+BANKS = 8
+TAB_PLANE = (4, 8)
+WI_PLANE = 12
+CAST_TILES = 4
+H_TILES = 4
+CTX_ON_SCALAR = 64
+SCALAR, VECTOR = "scalar", "vector"
 
 
 def tile_list_session_shift_recommender_kernel(tc, tab_words, tab_scales, offs, tab2_words, tab2_scales, offs2, ctx, w1,
                                                         w2_words, w2_scales, wg, wi_words, wi_scales, bi, out):
     nc = tc.nc
-    with ExitStack() as es:
-        keep = es.enter_context(tc.tile_pool(name="keep", bufs=1))
-        psum = es.enter_context(tc.psum_pool(name="psum", bufs=1))
-        eng = {"v": nc.vector, "s": nc.scalar, "g": nc.gpsimd}
-        sq = {"gpsimd": nc.gpsimd, "sync": nc.sync, "scalar": nc.scalar}[SCALEQ]
+    with ExitStack() as stack:
+        sbuf = stack.enter_context(tc.tile_pool(name="sbuf", bufs=1))
+        psum = stack.enter_context(tc.psum_pool(name="psum", bufs=1))
 
-        def kt(shape, dt, name):
-            return keep.tile(shape, dt, name=name, align_bytes=64)
+        def tile(shape, dtype, name):
+            return sbuf.tile(shape, dtype, name=name, align_bytes=64)
 
-        free_banks = [psum.tile([P, 512], F32, name="bank%d" % i) for i in range(8)]
-        rings = {}
+        def turn(ring):
+            ring.append(ring.pop(0))
+            return ring[-1]
 
-        def bank(kind):
-            return free_banks.pop(0)
+        free_banks = [psum.tile([P, WIDE], F32, name="bank%d" % i) for i in range(BANKS)]
 
-        def ring(name, n, shape, dt):
-            if name not in rings:
-                rings[name] = [kt(shape, dt, "%s_%d" % (name, i)) for i in range(n)]
-            rings[name].append(rings[name].pop(0))
-            return rings[name][-1]
+        idx = sbuf.tile([P, S // 16], U16, name="idx")
+        idx2 = sbuf.tile([P, S // 16], U16, name="idx2")
+        tab_w = [tile([P, T], I32, "tab_w%d" % a) for a in range(2)]
+        tab_s = tile([P, T // 4], I32, "tab_s")
+        tab2_w = tile([P, T2], I32, "tab2_w")
+        tab2_s = tile([P, T2 // 4], I32, "tab2_s")
+        w2_w_in = tile([P, H // 2], I32, "w2_w_in")
+        w2_s_in = tile([P, H // 4], I32, "w2_s_in")
+        w2_w = tile([P, 2 * H], U8, "w2_w")
+        w2_s = tile([P, H], U8, "w2_s")
+        wi_w = tile([P, 2, N], I32, "wi_w")
+        wi_s = tile([P, 2, N // 4], I32, "wi_s")
+        bias_rows = tile([P, P], F32, "bias_rows")
+        identity = tile([P, P], F32, "identity")
+        bias = tile([P, N // P], F32, "bias")
 
-        list1 = keep.tile([P, S // 16], U16, name="list1")
-        list2 = keep.tile([P, S // 16], U16, name="list2")
-        tabw = [kt([P, T], I32, "tabw%d" % a) for a in range(2)]
-        tabs = kt([P, T // 4], I32, "tabs")
-        tab2w = kt([P, T2], I32, "tab2w")
-        tab2s = kt([P, T2 // 4], I32, "tab2s")
-        w2raw = kt([P, H // 2], I32, "w2raw")
-        w2sraw = kt([P, H // 4], I32, "w2sraw")
-        w2c = kt([P, 2 * H], U8, "w2c")
-        w2s = kt([P, H], U8, "w2s")
-        wiw = kt([P, 2, N], I32, "wiw")
-        wis = kt([P, 2, N // 4], I32, "wis")
-        bias = kt([P, N // P], F32, "bias")
-        vw = [[kt([P, 512], U32, "vw%d%d" % (a, jh)) for jh in range(2)] for a in range(2)]
-        vs = [kt([P, 512], U8, "vs%d" % jh) for jh in range(2)]
-        v2w = [kt([P, 512], U32, "v2w%d" % jh) for jh in range(2)]
-        v2s = [kt([P, 512], U8, "v2s%d" % jh) for jh in range(2)]
-        hc = [kt([P, S], U32, "hc%d" % b) for b in range(2)]
-        hs = [kt([P, S], U8, "hs%d" % b) for b in range(2)]
-        src = {}
-        for b in range(2):
-            for a in range(2):
-                src["w1%d%d" % (a, b)] = w1[512 * a:512 * (a + 1), 512 * b:512 * (b + 1)]
-            src["wg%d" % b] = wg[:, 512 * b:512 * (b + 1)]
-        for x in range(S // CTXW):
-            src["ctx%d" % x] = ctx[:, CTXW * x:CTXW * (x + 1)]
-        whole = {"wg": wg, "ctx": ctx, "w10": w1[0:512, :], "w11": w1[512:1024, :]}
-        rawfull = {k: kt([P, 4, 1024], F32, "raw" + k) for k in FULL}
-        raw = {k: (rawfull[k[:-1]][:, :, int(k[-1]) * src[k].shape[1]:(int(k[-1]) + 1) * src[k].shape[1]] if k[:-1] in FULL
-                   else kt([P, 4, src[k].shape[1]], F32, "raw" + k)) for k in src}
-        codes = {k: kt([P, src[k].shape[1]], U32, "codes" + k) for k in src}
-        scal = {k: kt([P, src[k].shape[1]], U8, "scal" + k) for k in src}
-        spent = {}
-        for k in ("wg", "ctx"):
-            if k in FULL:
-                flat = rawfull[k][:].rearrange("p i c -> p (i c)")
-                spent[k] = [flat[:, 0:2048], flat[:, 2048:4096]]
+        picked = {(part, jh): tile([P, WIDE], U8 if part in ("tab_s", "tab2_s") else U32, "picked_%s%d" % (part, jh))
+                  for part in ("tab_w0", "tab_w1", "tab_s", "tab2_w", "tab2_s") for jh in range(2)}
+
+        wg_in = tile([P, PACK, H], F32, "wg_in")
+        ctx_in = tile([P, PACK, S], F32, "ctx_in")
+        piece_in = {("w1", a, b): tile([P, PACK, PASS], F32, "w1_in%d%d" % (a, b))[:] for b in range(2) for a in range(2)}
+        for x in range(2):
+            piece_in["wg", 0, x] = wg_in[:, :, PASS * x:PASS * (x + 1)]
+            piece_in["ctx", 0, x] = ctx_in[:, :, WIDE * x:WIDE * (x + 1)]
+        codes = {key: tile([P, PASS], U32, "codes_%s%d%d" % key) for key in piece_in}
+        scales = {key: tile([P, PASS], U8, "scales_%s%d%d" % key) for key in piece_in}
+        cast_ring = [tile([P, PACK * PASS], BF16, "cast%d" % i) for i in range(CAST_TILES)]
+
+        gate_ring = [tile([P, WIDE], F32, "gate%d" % i) for i in range(2 * S // NARROW)]
+        h_groups = {b: tile([P, PACK, WIDE], BF16, "h_groups%d" % b) for b in range(2)}
+        h_ring = [tile([P, NARROW, PACK], BF16, "h%d" % i) for i in range(H_TILES)]
+        h_codes = [tile([P, S], U32, "h_codes%d" % b) for b in range(2)]
+        h_scales = [tile([P, S], U8, "h_scales%d" % b) for b in range(2)]
+
+        ctx_flat = ctx_in[:].rearrange("p i j -> p (i j)")
+        score_ring = [ctx_flat[:, WIDE * u:WIDE * (u + 1)] for u in range(PACK * S // WIDE)]
+
+        cast_of, gate_of, bank_of, h_of = {}, {}, {}, {}
+
+        nc.vector.memset(tab2_s[:], 0)
+        nc.gpsimd.memset(w2_s_in[:], 0)
+        nc.vector.memset(tab_s[:], 0)
+        nc.gpsimd.memset(wi_s[:], 0)
+        nc.gpsimd.memset(bias_rows[:], 0.0)
+        make_identity(nc, identity[:])
+
+        def load_rows(dst, src):
+            nc.sync.dma_start(out=dst, in_=src.rearrange("(p i) c -> p i c", i=PACK))
+
+        def load_w1(a, b):
+            load_rows(piece_in["w1", a, b], w1[PASS * a:PASS * (a + 1), PASS * b:PASS * (b + 1)])
+
+        def load_words(dst, words):
+            nc.sync.dma_start(out=dst, in_=words.rearrange("p t i -> p (t i)").bitcast(I32))
+
+        def load_tab_scales(quad):
+            first = 32 * quad + TAB_PLANE[0]
+            nc.sync.dma_start(out=tab_s[first:first + 8, :], in_=tab_scales[:, 4 * quad:4 * quad + 4, :].bitcast(I32))
+
+        def load_scale_rows(dst, src, r):
+            nc.sync.dma_start(out=dst[r:P:32, :], in_=src[0, r:16:4, :].bitcast(I32))
+
+        def load_wi_scales(r):
+            nc.sync.dma_start(out=wi_s[WI_PLANE + r:P:32, :, :], in_=wi_scales.rearrange("a q e -> q a e")[r:16:4, :, :].bitcast(I32))
+
+        def load_bias():
+            rows = bi.rearrange("(c p) -> c p", p=P)
+            nc.sync.dma_start(out=bias_rows[0:4, :], in_=rows[0:4, :])
+            nc.sync.dma_start(out=bias_rows[4:6, :], in_=rows[4:6, :])
+
+        def turn_bias():
+            bank = free_banks.pop(0)
+            nc.tensor.transpose(bank[:, 0:P], bias_rows[:], identity[:])
+            nc.scalar.copy(bias[:], bank[:, 0:N // P])
+            free_banks.append(bank)
+
+        def scaled_copy(engine, dst, src, factor):
+            if engine == SCALAR:
+                nc.scalar.activation(out=dst, in_=src, func=ACT.Copy, scale=factor)
             else:
-                spent[k] = [raw[k + x][:].rearrange("p i c -> p (i c)") for x in "01"]
-        if ALIAS:
-            rings["ads"] = [x.rearrange("p (t j) -> p t j", t=4) for x in spent["wg"]] + [kt([P, 4, 512], F32, "ads2")[:]]
-        rings["res"] = [x[:, 512 * u:512 * u + 512] for x in spent["ctx"] for u in range(4)]
-        grouped, sig, pre, ads, hb = {}, {}, {}, {}, {}
+                nc.vector.tensor_scalar(dst, src, factor, None, ALU.mult)
 
-        nc.vector.memset(tab2s[:], 0)
-        nc.gpsimd.memset(w2sraw[:], 0)
-        nc.vector.memset(tabs[:], 0)
-        nc.gpsimd.memset(wis[:], 0)
-        brows = kt([P, P], F32, "brows")
-        ident = kt([P, P], F32, "ident")
-        nc.gpsimd.memset(brows[:], 0.0)
-        make_identity(nc, ident[:])
+        def cast_weight(name, a, b, low, high):
+            cast_of[name, a, b] = turn(cast_ring)
+            dst = cast_of[name, a, b][:].rearrange("p (t m i) -> p m i t", t=PACK, i=PACK)
+            src = piece_in[name, a, b].rearrange("p i (m t) -> p m i t", t=PACK)
+            factor = -1.0 if name == "w1" else 1.0
+            scaled_copy(low, dst[:, :, :, 0:2], src[:, :, :, 0:2], factor)
+            scaled_copy(high, dst[:, :, :, 2:4], src[:, :, :, 2:4], factor)
 
-        def biast():
-            bk = bank("b")
-            nc.tensor.transpose(bk[:, 0:P], brows[:], ident[:])
-            nc.scalar.copy(bias[:], bk[:, 0:N // P])
-            free_banks.append(bk)
+        def cast_ctx(jh, on_scalar):
+            cast_of["ctx", 0, jh] = turn(cast_ring)
+            dst = cast_of["ctx", 0, jh][:].rearrange("p (m x i) -> p m i x", x=4, i=PACK)
+            src = piece_in["ctx", 0, jh].rearrange("p i (m x) -> p m i x", x=4)
+            for engine, first, last in ((SCALAR, 0, on_scalar // 4), (VECTOR, on_scalar // 4, WIDE // 4)):
+                if last > first:
+                    scaled_copy(engine, dst[:, first:last], src[:, first:last], 1.0)
 
-        def load(name):
-            if name in FULL:
-                nc.sync.dma_start(out=rawfull[name][:], in_=whole[name].rearrange("(p i) c -> p i c", i=4))
-            elif name in src:
-                nc.sync.dma_start(out=raw[name][:], in_=src[name].rearrange("(p i) c -> p i c", i=4))
-            elif name == "list1":
-                nc.sync.dma_start(list1[:], offs)
-            elif name == "list2":
-                nc.sync.dma_start(list2[:], offs2)
-            elif name == "tab0" or name == "tab1":
-                a = int(name[3])
-                nc.sync.dma_start(out=tabw[a][:], in_=tab_words[a].rearrange("p t i -> p (t i)").bitcast(I32))
-            elif name == "tab2":
-                nc.sync.dma_start(out=tab2w[:], in_=tab2_words[0].rearrange("p t i -> p (t i)").bitcast(I32))
-            elif name == "w2":
-                nc.sync.dma_start(out=w2raw[:], in_=w2_words[0].bitcast(I32))
-            elif name == "wi":
-                nc.sync.dma_start(out=wiw[:], in_=wi_words.rearrange("a p e i -> p a (e i)").bitcast(I32))
-            elif name.startswith("tabs"):
-                a, r = divmod(int(name[4]), 4)
-                if not QFORM:
-                    sq.dma_start(out=tabs[4 + 4 * a + r:P:32, :], in_=tab_scales[a, r:16:4, :].bitcast(I32))
-                elif a == 0:
-                    sq.dma_start(out=tabs[32 * r + 4:32 * r + 12, :], in_=tab_scales[:, 4 * r:4 * r + 4, :].bitcast(I32))
-            elif name.startswith("tab2s"):
-                r = int(name[5])
-                sq.dma_start(out=tab2s[r:P:32, :], in_=tab2_scales[0, r:16:4, :].bitcast(I32))
-            elif name.startswith("w2s"):
-                r = int(name[3])
-                nc.sync.dma_start(out=w2sraw[r:P:32, :], in_=w2_scales[0, r:16:4, :].bitcast(I32))
-            elif name.startswith("wis"):
-                r = int(name[3])
-                nc.sync.dma_start(out=wis[12 + r:P:32, :, :], in_=wi_scales.rearrange("a q e -> q a e")[r:16:4, :, :].bitcast(I32))
-            elif name == "bias":
-                rows6 = bi.rearrange("(c p) -> c p", p=P)
-                nc.sync.dma_start(out=brows[0:4, :], in_=rows6[0:4, :])
-                nc.sync.dma_start(out=brows[4:6, :], in_=rows6[4:6, :])
+        def quantize(name, a, x):
+            nc.vector.quantize_mx(out=codes[name, a, x][:].bitcast(FP8X4), scales=scales[name, a, x][:], in_=cast_of[name, a, x][:])
 
-        def cast(name, shares):
-            width = src[name].shape[1]
-            g = ring("grouped", GBUFS, [P, 2048], BF16)[:, 0:4 * width]
-            grouped[name] = g
-            if name.startswith("w"):
-                o = g[:].rearrange("p (t m i) -> p m i t", t=4, i=4)
+        def gather(part, jh):
+            table = {"tab_w0": tab_w[0], "tab_w1": tab_w[1], "tab_s": tab_s, "tab2_w": tab2_w, "tab2_s": tab2_s}[part]
+            entries = (idx2 if part.startswith("tab2") else idx)[:, 32 * jh:32 * (jh + 1)]
+            window = table[:].bitcast(U8 if part in ("tab_s", "tab2_s") else U32)
+            nc.vector.tensor_copy(picked[part, jh][:], window.indirect(entries))
+
+        def regroup_w2():
+            nc.vector.tensor_copy(w2_w[:].bitcast(U16).rearrange("p (b t m) -> p b t m", b=2, t=PACK),
+                                  w2_w_in[:].bitcast(U16).rearrange("p (b m t) -> p b t m", b=2, t=PACK))
+            nc.vector.tensor_copy(w2_s[:].rearrange("p (b t m) -> p b t m", b=2, t=PACK),
+                                  w2_s_in[:].bitcast(U8).rearrange("p (b m t) -> p b t m", b=2, t=PACK))
+
+        def multiply(dst, term, b, t, j0, width, start, stop):
+            jh = j0 // WIDE
+            js = slice(j0 % WIDE, j0 % WIDE + width)
+            ms = slice(P * t, P * (t + 1))
+            if term == "c":
+                lhs, lhs_s = codes["wg", 0, b][:, ms].bitcast(FP8X4), scales["wg", 0, b][:, ms]
+                rhs, rhs_s = codes["ctx", 0, jh][:, js], scales["ctx", 0, jh][:, js]
+            elif term == "d":
+                col = PASS * b + P * t
+                lhs, lhs_s = w2_w[:, 2 * col:2 * (col + P)].bitcast(FP4X4), w2_s[:, col:col + P]
+                rhs, rhs_s = picked["tab2_w", jh][:, js], picked["tab2_s", jh][:, js]
             else:
-                o = g[:].rearrange("p (m t i) -> p m i t", t=4, i=4)
-            i_ = raw[name][:].rearrange("p i (m t) -> p m i t", t=4)
-            sign = -1.0 if name.startswith("w1") else 1.0
-            m0 = 0
-            for e, m1 in shares:
-                if name.startswith("w"):
-                    oo, ii = o[:, :, :, m0 // 32:m1 // 32], i_[:, :, :, m0 // 32:m1 // 32]
-                else:
-                    oo, ii = o[:, m0 * width // 512:m1 * width // 512], i_[:, m0 * width // 512:m1 * width // 512]
-                if e == "s":
-                    nc.scalar.activation(out=oo, in_=ii, func=ACT.Copy, scale=sign)
-                elif e == "g":
-                    nc.gpsimd.tensor_scalar(oo, ii, sign, 0.0, ALU.mult, ALU.add)
-                else:
-                    nc.vector.tensor_scalar(oo, ii, sign, None, ALU.mult)
-                m0 = m1
+                a = ("a0", "a1").index(term)
+                lhs, lhs_s = codes["w1", a, b][:, ms].bitcast(FP8X4), scales["w1", a, b][:, ms]
+                rhs, rhs_s = picked["tab_w%d" % a, jh][:, js], picked["tab_s", jh][TAB_PLANE[a]:P, js]
+            nc.tensor.matmul_mx(out=dst, lhsT=lhs, lhsT_scale=lhs_s, rhs=rhs.bitcast(FP8X4), rhs_scale=rhs_s, start=start, stop=stop)
 
-        def quant(name):
-            nc.vector.quantize_mx(out=codes[name][:].bitcast(FP8X4), scales=scal[name][:], in_=grouped[name][:])
+        def gate_narrow(b, q):
+            bank = free_banks.pop(0)
+            for t in range(PACK):
+                multiply(bank[:, NARROW * t:NARROW * (t + 1)], "c", b, t, NARROW * q, NARROW, True, True)
+            gate_of["narrow", b, q] = turn(gate_ring)[:].rearrange("p (j t) -> p j t", t=PACK)
+            nc.scalar.activation(out=gate_of["narrow", b, q], in_=bank[:].rearrange("p (t j) -> p j t", t=PACK), func=ACT.Sigmoid)
+            free_banks.append(bank)
 
-        def gather(which, jh):
-            cols = slice(32 * jh, 32 * jh + 32)
-            if which == "tabs":
-                nc.vector.tensor_copy(vs[jh][:], tabs[:].bitcast(U8).indirect(list1[:, cols]))
-            elif which == "tab2s":
-                nc.vector.tensor_copy(v2s[jh][:], tab2s[:].bitcast(U8).indirect(list2[:, cols]))
-            elif which == "tab2":
-                nc.vector.tensor_copy(v2w[jh][:], tab2w[:].bitcast(U32).indirect(list2[:, cols]))
-            else:
-                a = int(which[3])
-                nc.vector.tensor_copy(vw[a][jh][:], tabw[a][:].bitcast(U32).indirect(list1[:, cols]))
+        def sum_narrow(b, q):
+            bank = bank_of["narrow", b, q] = free_banks.pop(0)
+            for t in range(PACK):
+                for term in ("d", "a0", "a1"):
+                    multiply(bank[:, NARROW * t:NARROW * (t + 1)], term, b, t, NARROW * q, NARROW, term == "d", term == "a1")
 
-        def perm():
-            nc.vector.tensor_copy(w2c[:].bitcast(U16).rearrange("p (b t m) -> p b t m", b=2, t=4),
-                                  w2raw[:].bitcast(U16).rearrange("p (b m t) -> p b t m", b=2, t=4))
-            nc.vector.tensor_copy(w2s[:].rearrange("p (b t m) -> p b t m", b=2, t=4),
-                                  w2sraw[:].bitcast(U8).rearrange("p (b m t) -> p b t m", b=2, t=4))
+        def shift_narrow(b, q):
+            bank = bank_of["narrow", b, q]
+            h_of[b, q] = turn(h_ring)
+            nc.vector.scalar_tensor_tensor(h_of[b, q][:], bank[:].rearrange("p (t j) -> p j t", t=PACK), -1.0,
+                                           gate_of["narrow", b, q], ALU.mult, ALU.mult)
+            free_banks.append(bank)
 
-        def mm(o, which, b, t, j0, n, start, stop):
-            jh, js = j0 // 512, slice(j0 % 512, j0 % 512 + n)
-            ms = slice(128 * t, 128 * t + 128)
-            if which == "d":
-                c0 = 512 * b + 128 * t
-                args = (w2c[:, 2 * c0:2 * c0 + 256].bitcast(FP4X4), w2s[:, c0:c0 + 128], v2w[jh][:, js].bitcast(FP8X4), v2s[jh][:, js])
-            elif which == "c":
-                x = "ctx%d" % (j0 // CTXW)
-                xs = slice(j0 % CTXW, j0 % CTXW + n)
-                args = (codes["wg%d" % b][:, ms].bitcast(FP8X4), scal["wg%d" % b][:, ms], codes[x][:, xs].bitcast(FP8X4), scal[x][:, xs])
-            else:
-                a = int(which[1])
-                w = "w1%d%d" % (a, b)
-                args = (codes[w][:, ms].bitcast(FP8X4), scal[w][:, ms], vw[a][jh][:, js].bitcast(FP8X4), vs[jh][4 + 4 * a:P, js])
-            nc.tensor.matmul_mx(out=o, lhsT=args[0], lhsT_scale=args[1], rhs=args[2], rhs_scale=args[3], start=start, stop=stop)
+        def gate_wide(b, jh, t):
+            bank = free_banks.pop(0)
+            multiply(bank[:], "c", b, t, WIDE * jh, WIDE, True, True)
+            gate_of["wide", b, jh, t] = turn(gate_ring)[:]
+            nc.scalar.activation(out=gate_of["wide", b, jh, t], in_=bank[:], func=ACT.Sigmoid)
+            free_banks.append(bank)
 
-        def cdir(b, q):
-            bk = bank("c")
-            for t in range(4):
-                mm(bk[:, 128 * t:128 * t + 128], "c", b, t, 128 * q, 128, True, True)
-            sg = ring("sig", SIGBUFS, [P, 128, 4], F32)
-            sig[b, q] = sg
-            nc.scalar.activation(out=sg[:], in_=bk[:].rearrange("p (t j) -> p j t", t=4), func=ACT.Sigmoid)
-            free_banks.append(bk)
-
-        def admm(b, q):
-            bk = bank("ad")
-            pre[b, q] = bk
-            for t in range(4):
-                for n_, which in enumerate(("d", "a0", "a1")):
-                    mm(bk[:, 128 * t:128 * t + 128], which, b, t, 128 * q, 128, n_ == 0, n_ == 2)
-
-        def addir(b, q):
-            bk = pre[b, q]
-            h = ring("hb", HBUFS, [P, 128, 4], BF16)
-            hb[b, q] = h
-            nc.vector.scalar_tensor_tensor(h[:], bk[:].rearrange("p (t j) -> p j t", t=4), -1.0, sig[b, q][:], ALU.mult, ALU.mult)
-            free_banks.append(bk)
-
-        def hq(b, q):
-            js = slice(128 * q, 128 * q + 128)
-            nc.vector.quantize_mx(out=hc[b][:, js].bitcast(FP8X4), scales=hs[b][:, js], in_=hb[b, q][:].rearrange("p j t -> p (j t)"))
-
-        def prepass(b, jh, which, start, stop):
-            for t in range(4):
+        def sum_wide(b, jh, term, start, stop):
+            for t in range(PACK):
                 if start:
-                    pre[b, jh, t] = bank("ad")
-                mm(pre[b, jh, t][:], which, b, t, 512 * jh, 512, start, stop)
+                    bank_of["wide", b, jh, t] = free_banks.pop(0)
+                multiply(bank_of["wide", b, jh, t][:], term, b, t, WIDE * jh, WIDE, start, stop)
 
-        def store(b, jh, engines):
-            ads[b, jh] = ring("ads", ABUFS, [P, 4, 512], F32)
-            for t in range(4):
-                if engines[t] == "s":
-                    nc.scalar.activation(out=ads[b, jh][:, t, :], in_=pre[b, jh, t][:], func=ACT.Copy, scale=-1.0)
-                else:
-                    nc.vector.tensor_scalar(ads[b, jh][:, t, :], pre[b, jh, t][:], -1.0, None, ALU.mult)
-                free_banks.append(pre[b, jh, t])
+        def shift_wide(b, jh, t):
+            bank = bank_of["wide", b, jh, t]
+            nc.vector.scalar_tensor_tensor(h_groups[b][:, t, :], bank[:], -1.0, gate_of["wide", b, jh, t], ALU.mult, ALU.mult)
+            free_banks.append(bank)
 
-        def hst(b, q, e):
-            h = ring("hb", HBUFS, [P, 128, 4], BF16)
-            hb[b, q] = h
-            j0 = 128 * q % 512
-            eng[e].tensor_tensor(h[:].rearrange("p (c x) t -> p c t x", x=4),
-                                 ads[b, q // 4][:, :, j0:j0 + 128].rearrange("p t (c x) -> p c t x", x=4),
-                                 sig[b, q][:].rearrange("p (c x) t -> p c t x", x=4), ALU.mult)
-
-        def cplan(b, jh, t):
-            bk = bank("c")
-            mm(bk[:], "c", b, t, 512 * jh, 512, True, True)
-            sg = ring("sig", SIGBUFS, [P, 128, 4], F32)
-            sig[b, jh, t] = sg
-            nc.scalar.activation(out=sg[:].rearrange("p j t -> p (j t)"), in_=bk[:], func=ACT.Sigmoid)
-            free_banks.append(bk)
-
-        def hplan(b, jh, t):
-            if t == 0:
-                ads[b, jh] = ring("hpl", 2, [P, 4, 512], BF16)
-            nc.vector.scalar_tensor_tensor(ads[b, jh][:, t, :], pre[b, jh, t][:], -1.0, sig[b, jh, t][:].rearrange("p j t -> p (j t)"),
-                                           ALU.mult, ALU.mult)
-            free_banks.append(pre[b, jh, t])
-
-        def inter(b, q, e):
-            h = ring("hb", HBUFS, [P, 128, 4], BF16)
-            hb[b, q] = h
-            j0 = 128 * q % 512
-            o = h[:].rearrange("p (c x) t -> p c t x", x=4)
-            i_ = ads[b, q // 4][:, :, j0:j0 + 128].rearrange("p t (c x) -> p c t x", x=4)
-            if e == "g":
-                nc.gpsimd.tensor_scalar(o, i_, 1.0, 0.0, ALU.mult, ALU.add)
-            elif e == "s":
-                nc.scalar.copy(o, i_)
+        def interleave(b, q, engine):
+            h_of[b, q] = turn(h_ring)
+            j0 = NARROW * q % WIDE
+            dst = h_of[b, q][:].rearrange("p (m x) t -> p m t x", x=4)
+            src = h_groups[b][:, :, j0:j0 + NARROW].rearrange("p t (m x) -> p m t x", x=4)
+            if engine == SCALAR:
+                nc.scalar.copy(dst, src)
             else:
-                nc.vector.tensor_copy(o, i_)
+                nc.vector.tensor_copy(dst, src)
 
-        def ystage(j0, n, engines, group):
-            js = slice(j0, j0 + n)
-            per_bank = group
-            for c0 in range(0, 6, group):
-                res = ring("res", YBUFS, [P, 512], F32)[:, 0:group * n].rearrange("p (c j) -> p c j", c=group)
-                for c in range(c0, c0 + group):
-                    if c % per_bank == 0:
-                        bk = bank("y")
-                    o = bk[:, (c % per_bank) * n:(c % per_bank + 1) * n]
-                    for b in range(2):
-                        nc.tensor.matmul_mx(out=o, lhsT=wiw[:, b, 128 * c:128 * c + 128].bitcast(FP8X4),
-                                            lhsT_scale=wis[12:P, b, :].bitcast(U8)[:, 128 * c:128 * c + 128],
-                                            rhs=hc[b][:, js].bitcast(FP8X4), rhs_scale=hs[b][:, js], start=b == 0, stop=b == 1)
-                    if engines[c] == "s":
-                        nc.scalar.activation(out=res[:, c - c0, :], in_=o, func=ACT.Identity, bias=bias[:, c:c + 1])
-                    else:
-                        nc.vector.tensor_scalar(res[:, c - c0, :], o, bias[:, c:c + 1], None, ALU.add)
-                    if c % per_bank == per_bank - 1:
-                        free_banks.append(bk)
-                nc.sync.dma_start(out=out.rearrange("(c p) j -> p c j", p=P)[:, c0:c0 + group, js], in_=res[:])
+        def quantize_h(b, q):
+            js = slice(NARROW * q, NARROW * (q + 1))
+            nc.vector.quantize_mx(out=h_codes[b][:, js].bitcast(FP8X4), scales=h_scales[b][:, js],
+                                  in_=h_of[b, q][:].rearrange("p j t -> p (j t)"))
 
-        fns = dict(load=load, cast=cast, quant=quant, gather=gather, perm=perm, c=cdir, ad=addir, hq=hq, pre=prepass, store=store,
-                   hst=hst, y=ystage, biast=biast, adm=admm, cp=cplan, hp=hplan, il=inter)
-        for step in PLAN:
-            fns[step[0]](*step[1:])
+        def score(jh, engines):
+            js = slice(WIDE * jh, WIDE * (jh + 1))
+            for c, engine in enumerate(engines):
+                items = slice(P * c, P * (c + 1))
+                staged = turn(score_ring)
+                bank = free_banks.pop(0)
+                for b in range(2):
+                    nc.tensor.matmul_mx(out=bank[:], lhsT=wi_w[:, b, items].bitcast(FP8X4),
+                                        lhsT_scale=wi_s[WI_PLANE:P, b, :].bitcast(U8)[:, items],
+                                        rhs=h_codes[b][:, js].bitcast(FP8X4), rhs_scale=h_scales[b][:, js], start=b == 0, stop=b == 1)
+                if engine == SCALAR:
+                    nc.scalar.activation(out=staged, in_=bank[:], func=ACT.Identity, bias=bias[:, c:c + 1])
+                else:
+                    nc.vector.tensor_scalar(staged, bank[:], bias[:, c:c + 1], None, ALU.add)
+                free_banks.append(bank)
+                nc.sync.dma_start(out=out[items, js], in_=staged)
+
+        nc.sync.dma_start(idx2[:], offs2)
+        nc.sync.dma_start(idx[:], offs)
+        load_tab_scales(0)
+        load_scale_rows(tab2_s, tab2_scales, 0)
+        load_rows(ctx_in[:], ctx)
+        load_scale_rows(tab2_s, tab2_scales, 1)
+        load_scale_rows(w2_s_in, w2_scales, 0)
+        load_tab_scales(1)
+        load_rows(wg_in[:], wg)
+        nc.sync.dma_start(out=w2_w_in[:], in_=w2_words[0].bitcast(I32))
+        load_words(tab2_w[:], tab2_words[0])
+        load_w1(0, 1)
+        for r in (1, 2, 3):
+            load_scale_rows(w2_s_in, w2_scales, r)
+        load_scale_rows(tab2_s, tab2_scales, 2)
+        load_tab_scales(2)
+        load_tab_scales(3)
+        load_w1(1, 1)
+        load_scale_rows(tab2_s, tab2_scales, 3)
+        load_words(tab_w[1][:], tab_words[1])
+        load_words(tab_w[0][:], tab_words[0])
+        load_w1(0, 0)
+        load_wi_scales(0)
+        load_w1(1, 0)
+        load_bias()
+        load_wi_scales(1)
+        load_wi_scales(2)
+        nc.sync.dma_start(out=wi_w[:], in_=wi_words.rearrange("a p e i -> p a (e i)").bitcast(I32))
+        load_wi_scales(3)
+
+
+        cast_weight("wg", 0, 0, SCALAR, VECTOR)
+        cast_ctx(0, 0)
+        quantize("ctx", 0, 0)
+        cast_ctx(1, CTX_ON_SCALAR)
+        quantize("wg", 0, 0)
+        quantize("ctx", 0, 1)
+        cast_weight("wg", 0, 1, SCALAR, VECTOR)
+        quantize("wg", 0, 1)
+        for b in range(2):
+            for t in range(PACK):
+                gate_wide(b, 0, t)
+        for q in range(4, 8):
+            gate_narrow(1, q)
+
+        regroup_w2()
+        for part in ("tab_s", "tab2_w", "tab2_s"):
+            for jh in range(2):
+                gather(part, jh)
+        cast_weight("w1", 0, 1, VECTOR, VECTOR)
+        quantize("w1", 0, 1)
+        cast_weight("w1", 1, 1, SCALAR, VECTOR)
+        quantize("w1", 1, 1)
+        for part in ("tab_w1", "tab_w0"):
+            for jh in range(2):
+                gather(part, jh)
+        cast_weight("w1", 0, 0, SCALAR, SCALAR)
+        sum_narrow(1, 4)
+        shift_narrow(1, 4)
+        cast_weight("w1", 1, 0, SCALAR, VECTOR)
+        quantize("w1", 0, 0)
+        for q in range(4, 8):
+            gate_narrow(0, q)
+
+        sum_wide(0, 0, "d", True, False)
+        sum_wide(1, 0, "a1", True, False)
+        sum_wide(1, 0, "d", False, False)
+        sum_wide(1, 0, "a0", False, True)
+        shift_wide(1, 0, 0)
+        shift_wide(1, 0, 1)
+        sum_narrow(1, 5)
+        shift_wide(1, 0, 2)
+        sum_narrow(1, 6)
+        shift_wide(1, 0, 3)
+        quantize("w1", 1, 0)
+        sum_wide(0, 0, "a0", False, False)
+        sum_wide(0, 0, "a1", False, True)
+        shift_narrow(1, 5)
+        quantize_h(1, 4)
+        interleave(1, 0, SCALAR)
+        interleave(1, 1, SCALAR)
+        quantize_h(1, 0)
+        quantize_h(1, 5)
+        for t in range(PACK):
+            shift_wide(0, 0, t)
+        turn_bias()
+
+        interleave(1, 2, SCALAR)
+        quantize_h(1, 1)
+        sum_narrow(0, 4)
+        shift_narrow(0, 4)
+        sum_narrow(0, 5)
+        interleave(1, 3, SCALAR)
+        sum_narrow(1, 7)
+        sum_narrow(0, 6)
+        interleave(0, 0, SCALAR)
+        quantize_h(1, 2)
+        interleave(0, 1, SCALAR)
+        quantize_h(1, 3)
+        sum_narrow(0, 7)
+        quantize_h(0, 4)
+        interleave(0, 2, VECTOR)
+        interleave(0, 3, SCALAR)
+        quantize_h(0, 0)
+        quantize_h(0, 1)
+        shift_narrow(1, 6)
+        quantize_h(0, 2)
+        quantize_h(0, 3)
+
+        score(0, (SCALAR, SCALAR, SCALAR, SCALAR, SCALAR, VECTOR))
+        quantize_h(1, 6)
+        for b, q in ((0, 5), (1, 7), (0, 6), (0, 7)):
+            shift_narrow(b, q)
+        for b, q in ((0, 5), (1, 7), (0, 6), (0, 7)):
+            quantize_h(b, q)
+        score(1, (SCALAR, VECTOR, VECTOR, SCALAR, SCALAR, SCALAR))

from contextlib import ExitStack

import concourse.mybir as mybir
from concourse.masks import make_identity

K, K2, C, H, N, T, T2, S = 1024, 512, 512, 1024, 768, 4096, 2048, 1024
FLOPS = 2 * S * (K * H + K2 * H + C * H + H * N)

F32, BF16 = mybir.dt.float32, mybir.dt.bfloat16
I32, U32, U16, U8 = mybir.dt.int32, mybir.dt.uint32, mybir.dt.uint16, mybir.dt.uint8
FP8X4, FP4X4 = mybir.dt.float8_e4m3fn_x4, mybir.dt.float4_e2m1fn_x4
ACT, ALU = mybir.ActivationFunctionType, mybir.AluOpType

P = 128
PACK = 4
PASS = P * PACK
WIDE = 512
NARROW = 128
BANKS = 8
TAB_PLANE = (4, 8)
WI_PLANE = 12
CAST_TILES = 4
H_TILES = 4
CTX_ON_SCALAR = 64
SCALAR, VECTOR = "scalar", "vector"


def tile_list_session_shift_recommender_kernel(tc, tab_words, tab_scales, offs, tab2_words, tab2_scales, offs2, ctx, w1,
                                                        w2_words, w2_scales, wg, wi_words, wi_scales, bi, out):
    nc = tc.nc
    with ExitStack() as stack:
        sbuf = stack.enter_context(tc.tile_pool(name="sbuf", bufs=1))
        psum = stack.enter_context(tc.psum_pool(name="psum", bufs=1))

        def tile(shape, dtype, name):
            return sbuf.tile(shape, dtype, name=name, align_bytes=64)

        def turn(ring):
            ring.append(ring.pop(0))
            return ring[-1]

        free_banks = [psum.tile([P, WIDE], F32, name="bank%d" % i) for i in range(BANKS)]

        idx = sbuf.tile([P, S // 16], U16, name="idx")
        idx2 = sbuf.tile([P, S // 16], U16, name="idx2")
        tab_w = [tile([P, T], I32, "tab_w%d" % a) for a in range(2)]
        tab_s = tile([P, T // 4], I32, "tab_s")
        tab2_w = tile([P, T2], I32, "tab2_w")
        tab2_s = tile([P, T2 // 4], I32, "tab2_s")
        w2_w_in = tile([P, H // 2], I32, "w2_w_in")
        w2_s_in = tile([P, H // 4], I32, "w2_s_in")
        w2_w = tile([P, 2 * H], U8, "w2_w")
        w2_s = tile([P, H], U8, "w2_s")
        wi_w = tile([P, 2, N], I32, "wi_w")
        wi_s = tile([P, 2, N // 4], I32, "wi_s")
        bias_rows = tile([P, P], F32, "bias_rows")
        identity = tile([P, P], F32, "identity")
        bias = tile([P, N // P], F32, "bias")

        picked = {(part, jh): tile([P, WIDE], U8 if part in ("tab_s", "tab2_s") else U32, "picked_%s%d" % (part, jh))
                  for part in ("tab_w0", "tab_w1", "tab_s", "tab2_w", "tab2_s") for jh in range(2)}

        wg_in = tile([P, PACK, H], F32, "wg_in")
        ctx_in = tile([P, PACK, S], F32, "ctx_in")
        piece_in = {("w1", a, b): tile([P, PACK, PASS], F32, "w1_in%d%d" % (a, b))[:] for b in range(2) for a in range(2)}
        for x in range(2):
            piece_in["wg", 0, x] = wg_in[:, :, PASS * x:PASS * (x + 1)]
            piece_in["ctx", 0, x] = ctx_in[:, :, WIDE * x:WIDE * (x + 1)]
        codes = {key: tile([P, PASS], U32, "codes_%s%d%d" % key) for key in piece_in}
        scales = {key: tile([P, PASS], U8, "scales_%s%d%d" % key) for key in piece_in}
        cast_ring = [tile([P, PACK * PASS], BF16, "cast%d" % i) for i in range(CAST_TILES)]

        gate_ring = [tile([P, WIDE], F32, "gate%d" % i) for i in range(2 * S // NARROW)]
        h_groups = {b: tile([P, PACK, WIDE], BF16, "h_groups%d" % b) for b in range(2)}
        h_ring = [tile([P, NARROW, PACK], BF16, "h%d" % i) for i in range(H_TILES)]
        h_codes = [tile([P, S], U32, "h_codes%d" % b) for b in range(2)]
        h_scales = [tile([P, S], U8, "h_scales%d" % b) for b in range(2)]

        ctx_flat = ctx_in[:].rearrange("p i j -> p (i j)")
        score_ring = [ctx_flat[:, WIDE * u:WIDE * (u + 1)] for u in range(PACK * S // WIDE)]

        cast_of, gate_of, bank_of, h_of = {}, {}, {}, {}

        nc.vector.memset(tab2_s[:], 0)
        nc.gpsimd.memset(w2_s_in[:], 0)
        nc.vector.memset(tab_s[:], 0)
        nc.gpsimd.memset(wi_s[:], 0)
        nc.gpsimd.memset(bias_rows[:], 0.0)
        make_identity(nc, identity[:])

        def load_rows(dst, src):
            nc.sync.dma_start(out=dst, in_=src.rearrange("(p i) c -> p i c", i=PACK))

        def load_w1(a, b):
            load_rows(piece_in["w1", a, b], w1[PASS * a:PASS * (a + 1), PASS * b:PASS * (b + 1)])

        def load_words(dst, words):
            nc.sync.dma_start(out=dst, in_=words.rearrange("p t i -> p (t i)").bitcast(I32))

        def load_tab_scales(quad):
            first = 32 * quad + TAB_PLANE[0]
            nc.sync.dma_start(out=tab_s[first:first + 8, :], in_=tab_scales[:, 4 * quad:4 * quad + 4, :].bitcast(I32))

        def load_scale_rows(dst, src, r):
            nc.sync.dma_start(out=dst[r:P:32, :], in_=src[0, r:16:4, :].bitcast(I32))

        def load_wi_scales(r):
            nc.sync.dma_start(out=wi_s[WI_PLANE + r:P:32, :, :], in_=wi_scales.rearrange("a q e -> q a e")[r:16:4, :, :].bitcast(I32))

        def load_bias():
            rows = bi.rearrange("(c p) -> c p", p=P)
            nc.sync.dma_start(out=bias_rows[0:4, :], in_=rows[0:4, :])
            nc.sync.dma_start(out=bias_rows[4:6, :], in_=rows[4:6, :])

        def turn_bias():
            bank = free_banks.pop(0)
            nc.tensor.transpose(bank[:, 0:P], bias_rows[:], identity[:])
            nc.scalar.copy(bias[:], bank[:, 0:N // P])
            free_banks.append(bank)

        def scaled_copy(engine, dst, src, factor):
            if engine == SCALAR:
                nc.scalar.activation(out=dst, in_=src, func=ACT.Copy, scale=factor)
            else:
                nc.vector.tensor_scalar(dst, src, factor, None, ALU.mult)

        def cast_weight(name, a, b, low, high):
            cast_of[name, a, b] = turn(cast_ring)
            dst = cast_of[name, a, b][:].rearrange("p (t m i) -> p m i t", t=PACK, i=PACK)
            src = piece_in[name, a, b].rearrange("p i (m t) -> p m i t", t=PACK)
            factor = -1.0 if name == "w1" else 1.0
            scaled_copy(low, dst[:, :, :, 0:2], src[:, :, :, 0:2], factor)
            scaled_copy(high, dst[:, :, :, 2:4], src[:, :, :, 2:4], factor)

        def cast_ctx(jh, on_scalar):
            cast_of["ctx", 0, jh] = turn(cast_ring)
            dst = cast_of["ctx", 0, jh][:].rearrange("p (m x i) -> p m i x", x=4, i=PACK)
            src = piece_in["ctx", 0, jh].rearrange("p i (m x) -> p m i x", x=4)
            for engine, first, last in ((SCALAR, 0, on_scalar // 4), (VECTOR, on_scalar // 4, WIDE // 4)):
                if last > first:
                    scaled_copy(engine, dst[:, first:last], src[:, first:last], 1.0)

        def quantize(name, a, x):
            nc.vector.quantize_mx(out=codes[name, a, x][:].bitcast(FP8X4), scales=scales[name, a, x][:], in_=cast_of[name, a, x][:])

        def gather(part, jh):
            table = {"tab_w0": tab_w[0], "tab_w1": tab_w[1], "tab_s": tab_s, "tab2_w": tab2_w, "tab2_s": tab2_s}[part]
            entries = (idx2 if part.startswith("tab2") else idx)[:, 32 * jh:32 * (jh + 1)]
            window = table[:].bitcast(U8 if part in ("tab_s", "tab2_s") else U32)
            nc.vector.tensor_copy(picked[part, jh][:], window.indirect(entries))

        def regroup_w2():
            nc.vector.tensor_copy(w2_w[:].bitcast(U16).rearrange("p (b t m) -> p b t m", b=2, t=PACK),
                                  w2_w_in[:].bitcast(U16).rearrange("p (b m t) -> p b t m", b=2, t=PACK))
            nc.vector.tensor_copy(w2_s[:].rearrange("p (b t m) -> p b t m", b=2, t=PACK),
                                  w2_s_in[:].bitcast(U8).rearrange("p (b m t) -> p b t m", b=2, t=PACK))

        def multiply(dst, term, b, t, j0, width, start, stop):
            jh = j0 // WIDE
            js = slice(j0 % WIDE, j0 % WIDE + width)
            ms = slice(P * t, P * (t + 1))
            if term == "c":
                lhs, lhs_s = codes["wg", 0, b][:, ms].bitcast(FP8X4), scales["wg", 0, b][:, ms]
                rhs, rhs_s = codes["ctx", 0, jh][:, js], scales["ctx", 0, jh][:, js]
            elif term == "d":
                col = PASS * b + P * t
                lhs, lhs_s = w2_w[:, 2 * col:2 * (col + P)].bitcast(FP4X4), w2_s[:, col:col + P]
                rhs, rhs_s = picked["tab2_w", jh][:, js], picked["tab2_s", jh][:, js]
            else:
                a = ("a0", "a1").index(term)
                lhs, lhs_s = codes["w1", a, b][:, ms].bitcast(FP8X4), scales["w1", a, b][:, ms]
                rhs, rhs_s = picked["tab_w%d" % a, jh][:, js], picked["tab_s", jh][TAB_PLANE[a]:P, js]
            nc.tensor.matmul_mx(out=dst, lhsT=lhs, lhsT_scale=lhs_s, rhs=rhs.bitcast(FP8X4), rhs_scale=rhs_s, start=start, stop=stop)

        def gate_narrow(b, q):
            bank = free_banks.pop(0)
            for t in range(PACK):
                multiply(bank[:, NARROW * t:NARROW * (t + 1)], "c", b, t, NARROW * q, NARROW, True, True)
            gate_of["narrow", b, q] = turn(gate_ring)[:].rearrange("p (j t) -> p j t", t=PACK)
            nc.scalar.activation(out=gate_of["narrow", b, q], in_=bank[:].rearrange("p (t j) -> p j t", t=PACK), func=ACT.Sigmoid)
            free_banks.append(bank)

        def sum_narrow(b, q):
            bank = bank_of["narrow", b, q] = free_banks.pop(0)
            for t in range(PACK):
                for term in ("d", "a0", "a1"):
                    multiply(bank[:, NARROW * t:NARROW * (t + 1)], term, b, t, NARROW * q, NARROW, term == "d", term == "a1")

        def shift_narrow(b, q):
            bank = bank_of["narrow", b, q]
            h_of[b, q] = turn(h_ring)
            nc.vector.scalar_tensor_tensor(h_of[b, q][:], bank[:].rearrange("p (t j) -> p j t", t=PACK), -1.0,
                                           gate_of["narrow", b, q], ALU.mult, ALU.mult)
            free_banks.append(bank)

        def gate_wide(b, jh, t):
            bank = free_banks.pop(0)
            multiply(bank[:], "c", b, t, WIDE * jh, WIDE, True, True)
            gate_of["wide", b, jh, t] = turn(gate_ring)[:]
            nc.scalar.activation(out=gate_of["wide", b, jh, t], in_=bank[:], func=ACT.Sigmoid)
            free_banks.append(bank)

        def sum_wide(b, jh, term, start, stop):
            for t in range(PACK):
                if start:
                    bank_of["wide", b, jh, t] = free_banks.pop(0)
                multiply(bank_of["wide", b, jh, t][:], term, b, t, WIDE * jh, WIDE, start, stop)

        def shift_wide(b, jh, t):
            bank = bank_of["wide", b, jh, t]
            nc.vector.scalar_tensor_tensor(h_groups[b][:, t, :], bank[:], -1.0, gate_of["wide", b, jh, t], ALU.mult, ALU.mult)
            free_banks.append(bank)

        def interleave(b, q, engine):
            h_of[b, q] = turn(h_ring)
            j0 = NARROW * q % WIDE
            dst = h_of[b, q][:].rearrange("p (m x) t -> p m t x", x=4)
            src = h_groups[b][:, :, j0:j0 + NARROW].rearrange("p t (m x) -> p m t x", x=4)
            if engine == SCALAR:
                nc.scalar.copy(dst, src)
            else:
                nc.vector.tensor_copy(dst, src)

        def quantize_h(b, q):
            js = slice(NARROW * q, NARROW * (q + 1))
            nc.vector.quantize_mx(out=h_codes[b][:, js].bitcast(FP8X4), scales=h_scales[b][:, js],
                                  in_=h_of[b, q][:].rearrange("p j t -> p (j t)"))

        def score(jh, engines):
            js = slice(WIDE * jh, WIDE * (jh + 1))
            for c, engine in enumerate(engines):
                items = slice(P * c, P * (c + 1))
                staged = turn(score_ring)
                bank = free_banks.pop(0)
                for b in range(2):
                    nc.tensor.matmul_mx(out=bank[:], lhsT=wi_w[:, b, items].bitcast(FP8X4),
                                        lhsT_scale=wi_s[WI_PLANE:P, b, :].bitcast(U8)[:, items],
                                        rhs=h_codes[b][:, js].bitcast(FP8X4), rhs_scale=h_scales[b][:, js], start=b == 0, stop=b == 1)
                if engine == SCALAR:
                    nc.scalar.activation(out=staged, in_=bank[:], func=ACT.Identity, bias=bias[:, c:c + 1])
                else:
                    nc.vector.tensor_scalar(staged, bank[:], bias[:, c:c + 1], None, ALU.add)
                free_banks.append(bank)
                nc.sync.dma_start(out=out[items, js], in_=staged)

        nc.sync.dma_start(idx2[:], offs2)
        nc.sync.dma_start(idx[:], offs)
        load_tab_scales(0)
        load_scale_rows(tab2_s, tab2_scales, 0)
        load_rows(ctx_in[:], ctx)
        load_scale_rows(tab2_s, tab2_scales, 1)
        load_scale_rows(w2_s_in, w2_scales, 0)
        load_tab_scales(1)
        load_rows(wg_in[:], wg)
        nc.sync.dma_start(out=w2_w_in[:], in_=w2_words[0].bitcast(I32))
        load_words(tab2_w[:], tab2_words[0])
        load_w1(0, 1)
        for r in (1, 2, 3):
            load_scale_rows(w2_s_in, w2_scales, r)
        load_scale_rows(tab2_s, tab2_scales, 2)
        load_tab_scales(2)
        load_tab_scales(3)
        load_w1(1, 1)
        load_scale_rows(tab2_s, tab2_scales, 3)
        load_words(tab_w[1][:], tab_words[1])
        load_words(tab_w[0][:], tab_words[0])
        load_w1(0, 0)
        load_wi_scales(0)
        load_w1(1, 0)
        load_bias()
        load_wi_scales(1)
        load_wi_scales(2)
        nc.sync.dma_start(out=wi_w[:], in_=wi_words.rearrange("a p e i -> p a (e i)").bitcast(I32))
        load_wi_scales(3)


        cast_weight("wg", 0, 0, SCALAR, VECTOR)
        cast_ctx(0, 0)
        quantize("ctx", 0, 0)
        cast_ctx(1, CTX_ON_SCALAR)
        quantize("wg", 0, 0)
        quantize("ctx", 0, 1)
        cast_weight("wg", 0, 1, SCALAR, VECTOR)
        quantize("wg", 0, 1)
        for b in range(2):
            for t in range(PACK):
                gate_wide(b, 0, t)
        for q in range(4, 8):
            gate_narrow(1, q)

        regroup_w2()
        for part in ("tab_s", "tab2_w", "tab2_s"):
            for jh in range(2):
                gather(part, jh)
        cast_weight("w1", 0, 1, VECTOR, VECTOR)
        quantize("w1", 0, 1)
        cast_weight("w1", 1, 1, SCALAR, VECTOR)
        quantize("w1", 1, 1)
        for part in ("tab_w1", "tab_w0"):
            for jh in range(2):
                gather(part, jh)
        cast_weight("w1", 0, 0, SCALAR, SCALAR)
        sum_narrow(1, 4)
        shift_narrow(1, 4)
        cast_weight("w1", 1, 0, SCALAR, VECTOR)
        quantize("w1", 0, 0)
        for q in range(4, 8):
            gate_narrow(0, q)

        sum_wide(0, 0, "d", True, False)
        sum_wide(1, 0, "a1", True, False)
        sum_wide(1, 0, "d", False, False)
        sum_wide(1, 0, "a0", False, True)
        shift_wide(1, 0, 0)
        shift_wide(1, 0, 1)
        sum_narrow(1, 5)
        shift_wide(1, 0, 2)
        sum_narrow(1, 6)
        shift_wide(1, 0, 3)
        quantize("w1", 1, 0)
        sum_wide(0, 0, "a0", False, False)
        sum_wide(0, 0, "a1", False, True)
        shift_narrow(1, 5)
        quantize_h(1, 4)
        interleave(1, 0, SCALAR)
        interleave(1, 1, SCALAR)
        quantize_h(1, 0)
        quantize_h(1, 5)
        for t in range(PACK):
            shift_wide(0, 0, t)
        turn_bias()

        interleave(1, 2, SCALAR)
        quantize_h(1, 1)
        sum_narrow(0, 4)
        shift_narrow(0, 4)
        sum_narrow(0, 5)
        interleave(1, 3, SCALAR)
        sum_narrow(1, 7)
        sum_narrow(0, 6)
        interleave(0, 0, SCALAR)
        quantize_h(1, 2)
        interleave(0, 1, SCALAR)
        quantize_h(1, 3)
        sum_narrow(0, 7)
        quantize_h(0, 4)
        interleave(0, 2, VECTOR)
        interleave(0, 3, SCALAR)
        quantize_h(0, 0)
        quantize_h(0, 1)
        shift_narrow(1, 6)
        quantize_h(0, 2)
        quantize_h(0, 3)

        score(0, (SCALAR, SCALAR, SCALAR, SCALAR, SCALAR, VECTOR))
        quantize_h(1, 6)
        for b, q in ((0, 5), (1, 7), (0, 6), (0, 7)):
            shift_narrow(b, q)
        for b, q in ((0, 5), (1, 7), (0, 6), (0, 7)):
            quantize_h(b, q)
        score(1, (SCALAR, VECTOR, VECTOR, SCALAR, SCALAR, SCALAR))
